import numpy as np
import ml_dtypes


def mxq(x, axis, fmt="e4m3"):
    dtype, down = {"e4m3": (ml_dtypes.float8_e4m3fn, 7), "e5m2": (ml_dtypes.float8_e5m2, 14)}[fmt]
    v = np.moveaxis(np.asarray(x, np.float32).astype(ml_dtypes.bfloat16).astype(np.float64), axis, -1)
    blocks = v.reshape(v.shape[:-1] + (-1, 32))
    amax = np.abs(blocks).max(-1, keepdims=True)
    byte = np.maximum(np.where(amax > 0, np.frexp(amax)[1] - 1 + 127, 0) - down, 1)
    scale = np.exp2(byte - 127.0)
    codes = (blocks / scale).astype(np.float32).astype(dtype).astype(np.float64)
    return np.moveaxis((codes * scale).reshape(v.shape), -1, axis)


WIDE = False


def mx_kscale(k):
    if not WIDE:
        return np.ones(k)
    levels = np.array([10, -10, 5, -5, 0])
    if k % 512:
        return np.exp2(np.random.permutation(np.resize(levels, k // 32))).repeat(32)
    a = np.empty((k // 512, 16))
    for p in range(k // 512):
        a[p, :8] = np.random.permutation(np.resize(levels, 8))
        for g in range(8):
            far = levels[np.abs(levels - a[p, g]) >= 10]
            a[p, g + 8] = far[np.random.randint(len(far))]
    return np.exp2(a.ravel()).repeat(32)


def f64(x):
    return np.asarray(x).astype(np.float64)


def striped(idx):
    return np.tile(idx.reshape(-1, 16).T, (8, 1)).astype(np.uint16)


def unstriped(offs):
    return offs[:16].T.reshape(-1).astype(np.int64)


def silu(v):
    return v / (1.0 + np.exp(-np.maximum(v, -700.0)))


K, T, E, C, H, N = 512, 768, 6, 128, 1024, 128


def by_expert(wq, xq):
    return np.concatenate([wq[e].T @ xq[:, e * C:(e + 1) * C] for e in range(E)], axis=1)


def setup_inputs():
    n = np.random.standard_normal
    s = mx_kscale(K)[:, None]
    u = mx_kscale(H)
    return {
        "xT": (n((K, T)) * s).astype(np.float32),
        "w1": (n((E, K, H)) / np.sqrt(K) / s[None] * u[None, None, :]).astype(np.float32),
        "w2": (n((E, H, N)) / np.sqrt(H) / u[None, :, None]).astype(np.float32),
        "gate": np.tile(np.random.uniform(0.2, 1.0, E * C), (N, 1)).astype(np.float32),
        "offs": striped(np.random.permutation(T)[:E * C]),
        "dst": striped(np.random.permutation(T)[:E * C]),
    }


def reference(xT, w1, w2, gate, offs, dst):
    idx = unstriped(offs)
    xq = mxq(f64(xT)[:, idx], 0, "e4m3")
    h = silu(by_expert(mxq(f64(w1), 1, "e4m3"), xq))
    y = by_expert(mxq(f64(w2), 1, "e4m3"), mxq(h, 0, "e4m3"))
    out = np.zeros((N, T))
    out[:, unstriped(dst)] = f64(gate) * y
    return out

@@ -1,0 +1,223 @@
+from contextlib import ExitStack
+
+import concourse.mybir as mybir
+
+K, T, E, C, H, N = 512, 768, 6, 128, 1024, 128
+FLOPS = 2 * E * C * (K * H + H * N)
+
+F32 = mybir.dt.float32
+BF16 = mybir.dt.bfloat16
+U32 = mybir.dt.uint32
+U16 = mybir.dt.uint16
+U8 = mybir.dt.uint8
+FP8X4 = mybir.dt.float8_e4m3fn_x4
+SILU = mybir.ActivationFunctionType.Silu
+MULT = mybir.AluOpType.mult
+
+P = 128
+LATE = 2
+HALF = 512
+HALVES = H // HALF
+X_VECTOR = 512
+GATHER = 384
+STAGE = 2048
+
+
+def tile_moe_two_mlp_silu_kernel(tc, xT, w1, w2, gate, offs, dst, out):
+    nc = tc.nc
+    with ExitStack() as ctx:
+        lists = ctx.enter_context(tc.tile_pool(name="lists", bufs=1))
+        keep = ctx.enter_context(tc.tile_pool(name="keep", bufs=1))
+        ring = ctx.enter_context(tc.tile_pool(name="ring", bufs=3))
+        psum_h = ctx.enter_context(tc.psum_pool(name="psum_h", bufs=5))
+        psum_y = ctx.enter_context(tc.psum_pool(name="psum_y", bufs=2))
+
+        offs_sb = lists.tile([P, T // 16], U16, name="offs_sb")
+        dst_sb = lists.tile([P, T // 16], U16, name="dst_sb")
+
+        x_raw = keep.tile([P, 4, T], F32, name="x_raw")
+        w1_raw = [keep.tile([P, 4, H], F32, name=f"w1_raw{e}", align_bytes=64) for e in range(E)]
+        w2_raw = [keep.tile([P, HALVES, 4, N], F32, name=f"w2_raw{e}") for e in range(E)]
+        gate_a = keep.tile([P, 4 * C], F32, name="gate_a")
+        gate_b = keep.tile([P, 2 * C], F32, name="gate_b")
+
+        def load_w1(e):
+            nc.sync.dma_start(w1_raw[e][:], w1[e].rearrange("(p j) c -> p j c", j=4))
+
+        def load_w1_half(e, half):
+            cols = slice(half * HALF, (half + 1) * HALF)
+            nc.sync.dma_start(w1_raw[e][:, :, cols], w1[e].rearrange("(p j) c -> p j c", j=4)[:, :, cols])
+
+        def load_w2(e):
+            nc.sync.dma_start(w2_raw[e][:], w2[e].rearrange("(s p j) n -> p s j n", s=HALVES, j=4))
+
+        nc.sync.dma_start(x_raw[:], xT.rearrange("(p j) t -> p j t", j=4))
+        nc.sync.dma_start(offs_sb[:], offs)
+        for e in range(E):
+            if e == E - 1:
+                load_w1_half(e, 0)
+                load_w1_half(e, 1)
+            else:
+                load_w1(e)
+            if e == 0:
+                nc.sync.dma_start(dst_sb[:], dst)
+            if e < E - LATE:
+                load_w2(e)
+            if e == 0:
+                nc.sync.dma_start(gate_a[:], gate[:, : 4 * C])
+        for e in range(E - LATE, E):
+            load_w2(e)
+        nc.sync.dma_start(gate_b[:], gate[:, 4 * C :])
+
+        x_codes = keep.tile([P, T], U32, name="x_codes", align_bytes=64)
+        x_scales = keep.tile([P, T], U8, name="x_scales", align_bytes=64)
+        slot_codes = keep.tile([P, T], U32, name="slot_codes", align_bytes=64)
+        slot_scales = keep.tile([P, T], U8, name="slot_scales", align_bytes=64)
+        out_sb = keep.tile([P, T], F32, name="out_sb")
+        nc.gpsimd.memset(x_scales[:], 0)
+
+        warm = keep.tile([P, 1], F32, name="warm")
+        nc.vector.memset(warm[:], 0.0)
+        nc.scalar.activation(warm[:], warm[:], SILU)
+
+        def vcopy(dst_ap, src_ap):
+            nc.vector.tensor_copy(dst_ap, src_ap)
+
+        def scopy(dst_ap, src_ap):
+            nc.scalar.copy(dst_ap, src_ap)
+
+        def new_stage(name, width, bufs=2):
+            return ring.tile([P, width], BF16, name=name, align_bytes=64, bufs=bufs)
+
+        def quantize(codes, scales, stage, lo, width):
+            nc.vector.quantize_mx(out=codes.bitcast(FP8X4), scales=scales, in_=stage[:, lo : lo + width])
+
+        x_stage = keep.tile([P, 4 * T], BF16, name="x_stage", align_bytes=64)
+        for copy, lo, hi in ((vcopy, 0, X_VECTOR), (scopy, X_VECTOR, T)):
+            copy(
+                x_stage[:, 4 * lo : 4 * hi].rearrange("p (c i j) -> p c j i", i=4, j=4),
+                x_raw[:, :, lo:hi].rearrange("p j (c i) -> p c j i", i=4),
+            )
+            quantize(x_codes[:, lo:hi], x_scales[:, lo:hi], x_stage, 4 * lo, 4 * (hi - lo))
+
+        def gather(lo):
+            picked = offs_sb[:, lo // 16 : (lo + GATHER) // 16]
+            nc.vector.tensor_copy(slot_codes[:, lo : lo + GATHER], x_codes[:].indirect(picked))
+            nc.vector.tensor_copy(slot_scales[:, lo : lo + GATHER], x_scales[:].indirect(picked))
+
+        def copy_w1(copy, stage, e, half, t0=0, t1=4):
+            cols = slice(half * HALF, (half + 1) * HALF)
+            copy(
+                stage[:, HALF * t0 : HALF * t1].rearrange("p (t m j) -> p m j t", t=t1 - t0, j=4),
+                w1_raw[e][:, :, cols].rearrange("p j (m t) -> p m j t", t=4)[:, :, :, t0:t1],
+            )
+
+        def quantize_w1(stage, half, parts):
+            codes = ring.tile([P, HALF], U32, name=f"w1_codes{half}", align_bytes=64, bufs=2)
+            scales = ring.tile([P, HALF], U8, name=f"w1_scales{half}", align_bytes=64, bufs=2)
+            step = HALF // parts
+            for lo in range(0, HALF, step):
+                quantize(codes[:, lo : lo + step], scales[:, lo : lo + step], stage, 4 * lo, 4 * step)
+            return codes, scales
+
+        def first_layer(e, codes, scales):
+            slots = slice(e * C, (e + 1) * C)
+            acc = psum_h.tile([P, 4, C], F32, name="acc_h")
+            for t in range(4):
+                cols = slice(128 * t, 128 * (t + 1))
+                nc.tensor.matmul_mx(
+                    out=acc[:, t, :],
+                    lhsT=codes[:, cols].bitcast(FP8X4),
+                    lhsT_scale=scales[:, cols],
+                    rhs=slot_codes[:, slots].bitcast(FP8X4),
+                    rhs_scale=slot_scales[:, slots],
+                    start=True,
+                    stop=True,
+                )
+            return acc
+
+        def apply_silu(acc, stage):
+            nc.scalar.activation(
+                stage.rearrange("p (n t) -> p n t", t=4), acc[:].rearrange("p t n -> p n t"), SILU
+            )
+            return stage
+
+        def quantize_all(stage, name, width):
+            codes = ring.tile([P, width // 4], U32, name=f"{name}_codes", align_bytes=64, bufs=2)
+            scales = ring.tile([P, width // 4], U8, name=f"{name}_scales", align_bytes=64, bufs=2)
+            quantize(codes[:], scales[:], stage, 0, width)
+            return codes, scales
+
+        def copy_w2(copy, stage, e, s):
+            copy(
+                stage[:, 4 * N * s : 4 * N * (s + 1)].rearrange("p (c i j) -> p c j i", i=4, j=4),
+                w2_raw[e][:, s].rearrange("p j (c i) -> p c j i", i=4),
+            )
+
+        def second_layer(e, w2_q, h_q):
+            acc = psum_y.tile([P, C], F32, name="acc_y")
+            for s in range(HALVES):
+                nc.tensor.matmul_mx(
+                    out=acc[:],
+                    lhsT=w2_q[0][:, N * s : N * (s + 1)].bitcast(FP8X4),
+                    lhsT_scale=w2_q[1][:, N * s : N * (s + 1)],
+                    rhs=h_q[s][0][:].bitcast(FP8X4),
+                    rhs_scale=h_q[s][1][:],
+                    start=(s == 0),
+                    stop=(s == HALVES - 1),
+                )
+            return acc
+
+        def empty_y(e, acc):
+            y = w1_raw[(e + 2) % E][:, 0, :C]
+            gates = gate_a[:, e * C : (e + 1) * C] if e < 4 else gate_b[:, (e - 4) * C : (e - 3) * C]
+            nc.vector.tensor_tensor(y, acc[:], gates, MULT)
+            return y
+
+        def scatter(e, y):
+            places = dst_sb[:, e * C // 16 : (e + 1) * C // 16]
+            nc.vector.tensor_copy(out_sb[:].indirect(places), y)
+
+        for lo in range(0, T, GATHER):
+            gather(lo)
+        acc_h = {}
+        w2_stages = {}
+        acc_y = {}
+
+        def second_half(e):
+            own = new_stage("h_stage", 4 * C, bufs=3)
+            lent = w1_raw[(e + 1) % E][:, 0, HALF : HALF + 2 * C].bitcast(BF16)
+            h_b = apply_silu(acc_h[e, 1], own[:])
+            h_a = apply_silu(acc_h[e, 0], lent)
+            w2_q = quantize_all(w2_stages[e], "w2", HALVES * 4 * N)
+            hq_b = quantize_all(h_b, "hb", 4 * C)
+            hq_a = quantize_all(h_a, "ha", 4 * C)
+            acc_y[e] = second_layer(e, w2_q, (hq_a, hq_b))
+
+        for e in range(E):
+            s_stage = new_stage("s_stage", STAGE)
+            v_stage = new_stage("v_stage", STAGE)
+            if e < E - 1:
+                copy_w1(scopy, s_stage, e, 0)
+                copy_w1(vcopy, v_stage, e, 1)
+                parts = 1
+            else:
+                for half, stage in ((0, s_stage), (1, v_stage)):
+                    copy_w1(vcopy, stage, e, half, 0, 2)
+                    copy_w1(scopy, stage, e, half, 2, 4)
+                parts = 2
+            if e > 1:
+                y = empty_y(e - 2, acc_y[e - 2])
+            acc_h[e, 1] = first_layer(e, *quantize_w1(v_stage, 1, parts))
+            w2_stages[e] = new_stage("w2_stage", HALVES * 4 * N)
+            for s in range(HALVES):
+                copy_w2(scopy if e < E - 1 else vcopy, w2_stages[e], e, s)
+            acc_h[e, 0] = first_layer(e, *quantize_w1(s_stage, 0, parts))
+            if e > 0:
+                second_half(e - 1)
+            if e > 1:
+                scatter(e - 2, y)
+        second_half(E - 1)
+        for e in (E - 2, E - 1):
+            scatter(e, empty_y(e, acc_y[e]))
+        nc.sync.dma_start(out, out_sb[:])

@@ -1,9 +1,11 @@
 from contextlib import ExitStack
 
 import concourse.mybir as mybir
+from concourse.masks import make_identity
 
 K, T, E, C, H, N = 512, 768, 6, 128, 1024, 128
 FLOPS = 2 * E * C * (K * H + H * N)
+BYTES = 4 * (K * T + E * K * H + E * H * N + T + N * T) + 2 * 2 * 128 * (T // 16)
 
 F32 = mybir.dt.float32
 BF16 = mybir.dt.bfloat16
@@ -15,12 +17,13 @@ SILU = mybir.ActivationFunctionType.Silu
 MULT = mybir.AluOpType.mult
 
 P = 128
-LATE = 2
+EARLY = 4
 HALF = 512
 HALVES = H // HALF
-X_VECTOR = 512
+X_PIECE = 256
 GATHER = 384
-STAGE = 2048
+M_VECTOR = (80, 64)
+GATES = T // P
 
 
 def tile_moe_two_mlp_silu_kernel(tc, xT, w1, w2, gate, offs, dst, out):
@@ -29,52 +32,53 @@ def tile_moe_two_mlp_silu_kernel(tc, xT, w1, w2, gate, offs, dst, out):
         lists = ctx.enter_context(tc.tile_pool(name="lists", bufs=1))
         keep = ctx.enter_context(tc.tile_pool(name="keep", bufs=1))
         ring = ctx.enter_context(tc.tile_pool(name="ring", bufs=3))
-        psum_h = ctx.enter_context(tc.psum_pool(name="psum_h", bufs=5))
+        psum_h = ctx.enter_context(tc.psum_pool(name="psum_h", bufs=4))
         psum_y = ctx.enter_context(tc.psum_pool(name="psum_y", bufs=2))
+        psum_g = ctx.enter_context(tc.psum_pool(name="psum_g", bufs=2))
 
         offs_sb = lists.tile([P, T // 16], U16, name="offs_sb")
         dst_sb = lists.tile([P, T // 16], U16, name="dst_sb")
 
-        x_raw = keep.tile([P, 4, T], F32, name="x_raw")
-        w1_raw = [keep.tile([P, 4, H], F32, name=f"w1_raw{e}", align_bytes=64) for e in range(E)]
-        w2_raw = [keep.tile([P, HALVES, 4, N], F32, name=f"w2_raw{e}") for e in range(E)]
-        gate_a = keep.tile([P, 4 * C], F32, name="gate_a")
-        gate_b = keep.tile([P, 2 * C], F32, name="gate_b")
+        x_raw = [keep.tile([P, 4, X_PIECE], F32, name=f"x_raw{i}") for i in range(T // X_PIECE)]
+        w1_raw = {
+            (e, s): keep.tile([P, 4, HALF], F32, name=f"w1_raw{e}_{s}", align_bytes=64)
+            for e in range(E)
+            for s in range(HALVES)
+        }
+        w2_raw = [keep.tile([P, HALVES, 4, N], F32, name=f"w2_raw{e}", align_bytes=64) for e in range(E)]
+        first_stage = keep.tile([P, 4 * HALF], BF16, name="first_stage", align_bytes=64)
+        gate_row = first_stage[:, : 2 * GATES].bitcast(F32)
+        gate_sb = keep.tile([P, T], F32, name="gate_sb")
 
-        def load_w1(e):
-            nc.sync.dma_start(w1_raw[e][:], w1[e].rearrange("(p j) c -> p j c", j=4))
-
-        def load_w1_half(e, half):
-            cols = slice(half * HALF, (half + 1) * HALF)
-            nc.sync.dma_start(w1_raw[e][:, :, cols], w1[e].rearrange("(p j) c -> p j c", j=4)[:, :, cols])
+        def load_w1(e, s):
+            cols = slice(s * HALF, (s + 1) * HALF)
+            nc.sync.dma_start(w1_raw[e, s][:], w1[e].rearrange("(p j) c -> p j c", j=4)[:, :, cols])
 
         def load_w2(e):
             nc.sync.dma_start(w2_raw[e][:], w2[e].rearrange("(s p j) n -> p s j n", s=HALVES, j=4))
 
-        nc.sync.dma_start(x_raw[:], xT.rearrange("(p j) t -> p j t", j=4))
+        nc.sync.dma_start(gate_row, gate[0:1, :].rearrange("o (p m) -> (o p) m", m=GATES))
+        for i, piece in enumerate(x_raw):
+            nc.sync.dma_start(piece[:], xT.rearrange("(p j) t -> p j t", j=4)[:, :, i * X_PIECE : (i + 1) * X_PIECE])
         nc.sync.dma_start(offs_sb[:], offs)
         for e in range(E):
-            if e == E - 1:
-                load_w1_half(e, 0)
-                load_w1_half(e, 1)
-            else:
-                load_w1(e)
+            load_w1(e, 0)
+            load_w1(e, 1)
             if e == 0:
                 nc.sync.dma_start(dst_sb[:], dst)
-            if e < E - LATE:
+            if e < EARLY:
                 load_w2(e)
-            if e == 0:
-                nc.sync.dma_start(gate_a[:], gate[:, : 4 * C])
-        for e in range(E - LATE, E):
+        for e in range(EARLY, E):
             load_w2(e)
-        nc.sync.dma_start(gate_b[:], gate[:, 4 * C :])
 
         x_codes = keep.tile([P, T], U32, name="x_codes", align_bytes=64)
         x_scales = keep.tile([P, T], U8, name="x_scales", align_bytes=64)
         slot_codes = keep.tile([P, T], U32, name="slot_codes", align_bytes=64)
         slot_scales = keep.tile([P, T], U8, name="slot_scales", align_bytes=64)
         out_sb = keep.tile([P, T], F32, name="out_sb")
+        ident = keep.tile([P, P], F32, name="ident")
         nc.gpsimd.memset(x_scales[:], 0)
+        make_identity(nc, ident[:])
 
         warm = keep.tile([P, 1], F32, name="warm")
         nc.vector.memset(warm[:], 0.0)
@@ -86,41 +90,56 @@ def tile_moe_two_mlp_silu_kernel(tc, xT, w1, w2, gate, offs, dst, out):
         def scopy(dst_ap, src_ap):
             nc.scalar.copy(dst_ap, src_ap)
 
-        def new_stage(name, width, bufs=2):
-            return ring.tile([P, width], BF16, name=name, align_bytes=64, bufs=bufs)
+        def quantize(codes, scales, stage):
+            nc.vector.quantize_mx(out=codes.bitcast(FP8X4), scales=scales, in_=stage)
 
-        def quantize(codes, scales, stage, lo, width):
-            nc.vector.quantize_mx(out=codes.bitcast(FP8X4), scales=scales, in_=stage[:, lo : lo + width])
+        for copy, lo in ((scopy, 0), (scopy, 3)):
+            spread = psum_g.tile([P, 3, P], F32, name="spread")
+            for m in range(3):
+                nc.tensor.transpose(spread[:, m, :], gate_row[:, lo + m : lo + m + 1].to_broadcast([P, P]), ident[:])
+            copy(
+                gate_sb[:].rearrange("p (n m) -> p n m", m=GATES)[:, :, lo : lo + 3],
+                spread[:].rearrange("p m n -> p n m"),
+            )
 
         x_stage = keep.tile([P, 4 * T], BF16, name="x_stage", align_bytes=64)
-        for copy, lo, hi in ((vcopy, 0, X_VECTOR), (scopy, X_VECTOR, T)):
+        for i, copy in enumerate((vcopy, vcopy, vcopy)):
+            lo, hi = i * X_PIECE, (i + 1) * X_PIECE
             copy(
                 x_stage[:, 4 * lo : 4 * hi].rearrange("p (c i j) -> p c j i", i=4, j=4),
-                x_raw[:, :, lo:hi].rearrange("p j (c i) -> p c j i", i=4),
+                x_raw[i][:].rearrange("p j (c i) -> p c j i", i=4),
             )
-            quantize(x_codes[:, lo:hi], x_scales[:, lo:hi], x_stage, 4 * lo, 4 * (hi - lo))
+            quantize(x_codes[:, lo:hi], x_scales[:, lo:hi], x_stage[:, 4 * lo : 4 * hi])
 
-        def gather(lo):
+        for lo in range(0, T, GATHER):
             picked = offs_sb[:, lo // 16 : (lo + GATHER) // 16]
             nc.vector.tensor_copy(slot_codes[:, lo : lo + GATHER], x_codes[:].indirect(picked))
             nc.vector.tensor_copy(slot_scales[:, lo : lo + GATHER], x_scales[:].indirect(picked))
 
-        def copy_w1(copy, stage, e, half, t0=0, t1=4):
-            cols = slice(half * HALF, (half + 1) * HALF)
-            copy(
-                stage[:, HALF * t0 : HALF * t1].rearrange("p (t m j) -> p m j t", t=t1 - t0, j=4),
-                w1_raw[e][:, :, cols].rearrange("p j (m t) -> p m j t", t=4)[:, :, :, t0:t1],
-            )
-
-        def quantize_w1(stage, half, parts):
-            codes = ring.tile([P, HALF], U32, name=f"w1_codes{half}", align_bytes=64, bufs=2)
-            scales = ring.tile([P, HALF], U8, name=f"w1_scales{half}", align_bytes=64, bufs=2)
-            step = HALF // parts
-            for lo in range(0, HALF, step):
-                quantize(codes[:, lo : lo + step], scales[:, lo : lo + step], stage, 4 * lo, 4 * step)
+        def new_operand(name, words):
+            codes = ring.tile([P, words], U32, name=f"{name}_codes", align_bytes=64)
+            scales = ring.tile([P, words], U8, name=f"{name}_scales", align_bytes=64)
             return codes, scales
 
-        def first_layer(e, codes, scales):
+        def quantized(name, stage, words):
+            codes, scales = new_operand(name, words)
+            quantize(codes[:], scales[:], stage)
+            return codes, scales
+
+        def copy_w1(e, s, m_vector):
+            if (e, s) == (0, 0):
+                stage = first_stage
+            else:
+                stage = ring.tile([P, 4 * HALF], BF16, name="w1_stage", align_bytes=64)
+            to = stage[:].rearrange("p (t m j) -> p m j t", t=4, j=4)
+            source = w1_raw[e, s][:].rearrange("p j (m t) -> p m j t", t=4)
+            if m_vector > 0:
+                vcopy(to[:, :m_vector], source[:, :m_vector])
+            scopy(to[:, m_vector:], source[:, m_vector:])
+            return stage
+
+        def first_layer(e, stage, s):
+            codes, scales = quantized("w1", stage[:], HALF)
             slots = slice(e * C, (e + 1) * C)
             acc = psum_h.tile([P, 4, C], F32, name="acc_h")
             for t in range(4):
@@ -136,25 +155,21 @@ def tile_moe_two_mlp_silu_kernel(tc, xT, w1, w2, gate, offs, dst, out):
                 )
             return acc
 
-        def apply_silu(acc, stage):
-            nc.scalar.activation(
-                stage.rearrange("p (n t) -> p n t", t=4), acc[:].rearrange("p t n -> p n t"), SILU
-            )
+        def apply_silu(acc, over):
+            h = over.bitcast(BF16)
+            nc.scalar.activation(h.rearrange("p (n t) -> p n t", t=4), acc[:].rearrange("p t n -> p n t"), SILU)
+            return h
+
+        def copy_w2(e, shares):
+            staged = ring.tile([P, HALVES * 4 * N], BF16, name="w2_stage", align_bytes=64)
+            stage = staged[:]
+            to = stage.rearrange("p (s c i j) -> p s c j i", s=HALVES, i=4, j=4)
+            source = w2_raw[e][:].rearrange("p s j (c i) -> p s c j i", i=4)
+            for copy, passes in shares:
+                copy(to[:, passes], source[:, passes])
             return stage
 
-        def quantize_all(stage, name, width):
-            codes = ring.tile([P, width // 4], U32, name=f"{name}_codes", align_bytes=64, bufs=2)
-            scales = ring.tile([P, width // 4], U8, name=f"{name}_scales", align_bytes=64, bufs=2)
-            quantize(codes[:], scales[:], stage, 0, width)
-            return codes, scales
-
-        def copy_w2(copy, stage, e, s):
-            copy(
-                stage[:, 4 * N * s : 4 * N * (s + 1)].rearrange("p (c i j) -> p c j i", i=4, j=4),
-                w2_raw[e][:, s].rearrange("p j (c i) -> p c j i", i=4),
-            )
-
-        def second_layer(e, w2_q, h_q):
+        def second_layer(w2_q, h_q):
             acc = psum_y.tile([P, C], F32, name="acc_y")
             for s in range(HALVES):
                 nc.tensor.matmul_mx(
@@ -168,56 +183,51 @@ def tile_moe_two_mlp_silu_kernel(tc, xT, w1, w2, gate, offs, dst, out):
                 )
             return acc
 
-        def empty_y(e, acc):
-            y = w1_raw[(e + 2) % E][:, 0, :C]
-            gates = gate_a[:, e * C : (e + 1) * C] if e < 4 else gate_b[:, (e - 4) * C : (e - 3) * C]
-            nc.vector.tensor_tensor(y, acc[:], gates, MULT)
+        def times_gate(e, acc, over):
+            y = over[:, 2, :C]
+            nc.vector.tensor_tensor(y, acc[:], gate_sb[:, e * C : (e + 1) * C], MULT)
             return y
 
         def scatter(e, y):
             places = dst_sb[:, e * C // 16 : (e + 1) * C // 16]
             nc.vector.tensor_copy(out_sb[:].indirect(places), y)
 
-        for lo in range(0, T, GATHER):
-            gather(lo)
-        acc_h = {}
-        w2_stages = {}
-        acc_y = {}
+        def scalar_part(e, s):
+            return w1_raw[e, s][:, 0, 2 * C :]
 
-        def second_half(e):
-            own = new_stage("h_stage", 4 * C, bufs=3)
-            lent = w1_raw[(e + 1) % E][:, 0, HALF : HALF + 2 * C].bitcast(BF16)
-            h_b = apply_silu(acc_h[e, 1], own[:])
-            h_a = apply_silu(acc_h[e, 0], lent)
-            w2_q = quantize_all(w2_stages[e], "w2", HALVES * 4 * N)
-            hq_b = quantize_all(h_b, "hb", 4 * C)
-            hq_a = quantize_all(h_a, "ha", 4 * C)
-            acc_y[e] = second_layer(e, w2_q, (hq_a, hq_b))
-
+        acc_b, hq_a, hq_b, w2_q = {}, {}, {}, {}
+        last = E - 1
         for e in range(E):
-            s_stage = new_stage("s_stage", STAGE)
-            v_stage = new_stage("v_stage", STAGE)
-            if e < E - 1:
-                copy_w1(scopy, s_stage, e, 0)
-                copy_w1(vcopy, v_stage, e, 1)
-                parts = 1
-            else:
-                for half, stage in ((0, s_stage), (1, v_stage)):
-                    copy_w1(vcopy, stage, e, half, 0, 2)
-                    copy_w1(scopy, stage, e, half, 2, 4)
-                parts = 2
-            if e > 1:
-                y = empty_y(e - 2, acc_y[e - 2])
-            acc_h[e, 1] = first_layer(e, *quantize_w1(v_stage, 1, parts))
-            w2_stages[e] = new_stage("w2_stage", HALVES * 4 * N)
-            for s in range(HALVES):
-                copy_w2(scopy if e < E - 1 else vcopy, w2_stages[e], e, s)
-            acc_h[e, 0] = first_layer(e, *quantize_w1(s_stage, 0, parts))
+            stage = copy_w1(e, 0, M_VECTOR[0] if e > 0 else 0)
             if e > 0:
-                second_half(e - 1)
-            if e > 1:
-                scatter(e - 2, y)
-        second_half(E - 1)
-        for e in (E - 2, E - 1):
-            scatter(e, empty_y(e, acc_y[e]))
+                h_b = apply_silu(acc_b[e - 1], scalar_part(e, 0))
+            acc_a = first_layer(e, stage, 0)
+            if e > 0:
+                hq_b[e - 1] = quantized("hb", h_b, C)
+            if 0 < e <= EARLY:
+                acc_y = second_layer(w2_q[e - 1], (hq_a[e - 1], hq_b[e - 1]))
+            stage = copy_w1(e, 1, M_VECTOR[1])
+            if 0 < e <= EARLY:
+                y = times_gate(e - 1, acc_y, w1_raw[e, 1])
+            acc_b[e] = first_layer(e, stage, 1)
+            if 0 < e <= EARLY:
+                scatter(e - 1, y)
+            if e < EARLY:
+                w2_stage = copy_w2(e, [(scopy, slice(0, 2))])
+                h_a = apply_silu(acc_a, w2_raw[e][:, 0, 0:2, :].rearrange("p j n -> p (j n)"))
+                w2_q[e] = quantized("w2", w2_stage, HALVES * N)
+            else:
+                h_a = apply_silu(acc_a, scalar_part(e, 1))
+            hq_a[e] = quantized("ha", h_a, C)
+        shared = [(scopy, slice(0, 1)), (vcopy, slice(1, 2))]
+        w2_q[last - 1] = quantized("w2", copy_w2(last - 1, shared), HALVES * N)
+        acc_y = second_layer(w2_q[last - 1], (hq_a[last - 1], hq_b[last - 1]))
+        h_b = apply_silu(acc_b[last], scalar_part(last, 0))
+        w2_stage = copy_w2(last, shared)
+        y = times_gate(last - 1, acc_y, w1_raw[last, 1])
+        hq_b[last] = quantized("hb", h_b, C)
+        w2_q[last] = quantized("w2", w2_stage, HALVES * N)
+        scatter(last - 1, y)
+        acc_y = second_layer(w2_q[last], (hq_a[last], hq_b[last]))
+        scatter(last, times_gate(last, acc_y, w1_raw[last, 0]))
         nc.sync.dma_start(out, out_sb[:])

@@ -20,9 +20,10 @@ P = 128
 EARLY = 4
 HALF = 512
 HALVES = H // HALF
-X_PIECE = 256
+X_VECTOR = 512
 GATHER = 384
-M_VECTOR = (80, 64)
+M_VECTOR = 80
+M_VECTOR_FIRST = 64
 GATES = T // P
 
 
@@ -39,31 +40,24 @@ def tile_moe_two_mlp_silu_kernel(tc, xT, w1, w2, gate, offs, dst, out):
         offs_sb = lists.tile([P, T // 16], U16, name="offs_sb")
         dst_sb = lists.tile([P, T // 16], U16, name="dst_sb")
 
-        x_raw = [keep.tile([P, 4, X_PIECE], F32, name=f"x_raw{i}") for i in range(T // X_PIECE)]
-        w1_raw = {
-            (e, s): keep.tile([P, 4, HALF], F32, name=f"w1_raw{e}_{s}", align_bytes=64)
-            for e in range(E)
-            for s in range(HALVES)
-        }
+        x_raw = keep.tile([P, 4, T], F32, name="x_raw")
+        w1_raw = [keep.tile([P, 4, H], F32, name=f"w1_raw{e}") for e in range(E)]
         w2_raw = [keep.tile([P, HALVES, 4, N], F32, name=f"w2_raw{e}", align_bytes=64) for e in range(E)]
-        first_stage = keep.tile([P, 4 * HALF], BF16, name="first_stage", align_bytes=64)
-        gate_row = first_stage[:, : 2 * GATES].bitcast(F32)
+        x_stage = keep.tile([P, 4 * T], BF16, name="x_stage", align_bytes=64)
+        gate_row = keep.tile([P, GATES], F32, name="gate_row")
         gate_sb = keep.tile([P, T], F32, name="gate_sb")
 
-        def load_w1(e, s):
-            cols = slice(s * HALF, (s + 1) * HALF)
-            nc.sync.dma_start(w1_raw[e, s][:], w1[e].rearrange("(p j) c -> p j c", j=4)[:, :, cols])
+        def load_w1(e):
+            nc.sync.dma_start(w1_raw[e][:], w1[e].rearrange("(p j) c -> p j c", j=4))
 
         def load_w2(e):
             nc.sync.dma_start(w2_raw[e][:], w2[e].rearrange("(s p j) n -> p s j n", s=HALVES, j=4))
 
-        nc.sync.dma_start(gate_row, gate[0:1, :].rearrange("o (p m) -> (o p) m", m=GATES))
-        for i, piece in enumerate(x_raw):
-            nc.sync.dma_start(piece[:], xT.rearrange("(p j) t -> p j t", j=4)[:, :, i * X_PIECE : (i + 1) * X_PIECE])
+        nc.sync.dma_start(gate_row[:], gate[0:1, :].rearrange("o (p m) -> (o p) m", m=GATES))
+        nc.sync.dma_start(x_raw[:], xT.rearrange("(p j) t -> p j t", j=4))
         nc.sync.dma_start(offs_sb[:], offs)
         for e in range(E):
-            load_w1(e, 0)
-            load_w1(e, 1)
+            load_w1(e)
             if e == 0:
                 nc.sync.dma_start(dst_sb[:], dst)
             if e < EARLY:
@@ -102,12 +96,10 @@ def tile_moe_two_mlp_silu_kernel(tc, xT, w1, w2, gate, offs, dst, out):
                 spread[:].rearrange("p m n -> p n m"),
             )
 
-        x_stage = keep.tile([P, 4 * T], BF16, name="x_stage", align_bytes=64)
-        for i, copy in enumerate((vcopy, vcopy, vcopy)):
-            lo, hi = i * X_PIECE, (i + 1) * X_PIECE
+        for copy, lo, hi in ((vcopy, 0, X_VECTOR), (scopy, X_VECTOR, T)):
             copy(
                 x_stage[:, 4 * lo : 4 * hi].rearrange("p (c i j) -> p c j i", i=4, j=4),
-                x_raw[i][:].rearrange("p j (c i) -> p c j i", i=4),
+                x_raw[:, :, lo:hi].rearrange("p j (c i) -> p c j i", i=4),
             )
             quantize(x_codes[:, lo:hi], x_scales[:, lo:hi], x_stage[:, 4 * lo : 4 * hi])
 
@@ -127,14 +119,10 @@ def tile_moe_two_mlp_silu_kernel(tc, xT, w1, w2, gate, offs, dst, out):
             return codes, scales
 
         def copy_w1(e, s, m_vector):
-            if (e, s) == (0, 0):
-                stage = first_stage
-            else:
-                stage = ring.tile([P, 4 * HALF], BF16, name="w1_stage", align_bytes=64)
+            stage = ring.tile([P, 4 * HALF], BF16, name="w1_stage", align_bytes=64, bufs=4)
             to = stage[:].rearrange("p (t m j) -> p m j t", t=4, j=4)
-            source = w1_raw[e, s][:].rearrange("p j (m t) -> p m j t", t=4)
-            if m_vector > 0:
-                vcopy(to[:, :m_vector], source[:, :m_vector])
+            source = w1_raw[e][:, :, s * HALF : (s + 1) * HALF].rearrange("p j (m t) -> p m j t", t=4)
+            vcopy(to[:, :m_vector], source[:, :m_vector])
             scopy(to[:, m_vector:], source[:, m_vector:])
             return stage
 
@@ -155,10 +143,8 @@ def tile_moe_two_mlp_silu_kernel(tc, xT, w1, w2, gate, offs, dst, out):
                 )
             return acc
 
-        def apply_silu(acc, over):
-            h = over.bitcast(BF16)
+        def apply_silu(acc, h):
             nc.scalar.activation(h.rearrange("p (n t) -> p n t", t=4), acc[:].rearrange("p t n -> p n t"), SILU)
-            return h
 
         def copy_w2(e, shares):
             staged = ring.tile([P, HALVES * 4 * N], BF16, name="w2_stage", align_bytes=64)
@@ -176,15 +162,15 @@ def tile_moe_two_mlp_silu_kernel(tc, xT, w1, w2, gate, offs, dst, out):
                     out=acc[:],
                     lhsT=w2_q[0][:, N * s : N * (s + 1)].bitcast(FP8X4),
                     lhsT_scale=w2_q[1][:, N * s : N * (s + 1)],
-                    rhs=h_q[s][0][:].bitcast(FP8X4),
-                    rhs_scale=h_q[s][1][:],
+                    rhs=h_q[0][:, C * s : C * (s + 1)].bitcast(FP8X4),
+                    rhs_scale=h_q[1][:, C * s : C * (s + 1)],
                     start=(s == 0),
                     stop=(s == HALVES - 1),
                 )
             return acc
 
         def times_gate(e, acc, over):
-            y = over[:, 2, :C]
+            y = over[:, 2, HALF : HALF + C]
             nc.vector.tensor_tensor(y, acc[:], gate_sb[:, e * C : (e + 1) * C], MULT)
             return y
 
@@ -192,42 +178,32 @@ def tile_moe_two_mlp_silu_kernel(tc, xT, w1, w2, gate, offs, dst, out):
             places = dst_sb[:, e * C // 16 : (e + 1) * C // 16]
             nc.vector.tensor_copy(out_sb[:].indirect(places), y)
 
-        def scalar_part(e, s):
-            return w1_raw[e, s][:, 0, 2 * C :]
-
-        acc_b, hq_a, hq_b, w2_q = {}, {}, {}, {}
+        h_q, w2_q = {}, {}
         last = E - 1
         for e in range(E):
-            stage = copy_w1(e, 0, M_VECTOR[0] if e > 0 else 0)
-            if e > 0:
-                h_b = apply_silu(acc_b[e - 1], scalar_part(e, 0))
-            acc_a = first_layer(e, stage, 0)
-            if e > 0:
-                hq_b[e - 1] = quantized("hb", h_b, C)
+            share = M_VECTOR if e > 0 else M_VECTOR_FIRST
+            stages = [copy_w1(e, s, share) for s in range(HALVES)]
+            accs = [first_layer(e, stages[s], s) for s in range(HALVES)]
             if 0 < e <= EARLY:
-                acc_y = second_layer(w2_q[e - 1], (hq_a[e - 1], hq_b[e - 1]))
-            stage = copy_w1(e, 1, M_VECTOR[1])
-            if 0 < e <= EARLY:
-                y = times_gate(e - 1, acc_y, w1_raw[e, 1])
-            acc_b[e] = first_layer(e, stage, 1)
-            if 0 < e <= EARLY:
-                scatter(e - 1, y)
+                scatter(e - 1, times_gate(e - 1, acc_y, w1_raw[e]))
             if e < EARLY:
-                w2_stage = copy_w2(e, [(scopy, slice(0, 2))])
-                h_a = apply_silu(acc_a, w2_raw[e][:, 0, 0:2, :].rearrange("p j n -> p (j n)"))
-                w2_q[e] = quantized("w2", w2_stage, HALVES * N)
-            else:
-                h_a = apply_silu(acc_a, scalar_part(e, 1))
-            hq_a[e] = quantized("ha", h_a, C)
-        shared = [(scopy, slice(0, 1)), (vcopy, slice(1, 2))]
-        w2_q[last - 1] = quantized("w2", copy_w2(last - 1, shared), HALVES * N)
-        acc_y = second_layer(w2_q[last - 1], (hq_a[last - 1], hq_b[last - 1]))
-        h_b = apply_silu(acc_b[last], scalar_part(last, 0))
-        w2_stage = copy_w2(last, shared)
-        y = times_gate(last - 1, acc_y, w1_raw[last, 1])
-        hq_b[last] = quantized("hb", h_b, C)
-        w2_q[last] = quantized("w2", w2_stage, HALVES * N)
+                w2_q[e] = quantized("w2", copy_w2(e, [(scopy, slice(0, 2))]), HALVES * N)
+            if e == last:
+                w2_q[e - 1] = quantized("w2", copy_w2(e - 1, [(scopy, slice(0, 2))]), HALVES * N)
+                w2_q[e] = quantized("w2", copy_w2(e, [(vcopy, slice(0, 2))]), HALVES * N)
+                acc_y = second_layer(w2_q[e - 1], h_q[e - 1])
+            h = ring.tile([P, HALVES * 4 * C], BF16, name="h_stage", align_bytes=64)
+            for s in range(HALVES):
+                apply_silu(accs[s], h[:, 4 * C * s : 4 * C * (s + 1)])
+            if e < last:
+                h_q[e] = quantized("h", h[:], HALVES * C)
+            if e < EARLY:
+                acc_y = second_layer(w2_q[e], h_q[e])
+        codes, scales = new_operand("h", HALVES * C)
+        quantize(codes[:, :C], scales[:, :C], h[:, : 4 * C])
+        y = times_gate(last - 1, acc_y, w1_raw[last])
+        quantize(codes[:, C:], scales[:, C:], h[:, 4 * C :])
         scatter(last - 1, y)
-        acc_y = second_layer(w2_q[last], (hq_a[last], hq_b[last]))
-        scatter(last, times_gate(last, acc_y, w1_raw[last, 0]))
+        acc_y = second_layer(w2_q[last], (codes, scales))
+        scatter(last, times_gate(last, acc_y, w1_raw[0]))
         nc.sync.dma_start(out, out_sb[:])

@@ -98,8 +98,8 @@ def tile_moe_two_mlp_silu_kernel(tc, xT, w1, w2, gate, offs, dst, out):
 
         for copy, lo, hi in ((vcopy, 0, X_VECTOR), (scopy, X_VECTOR, T)):
             copy(
-                x_stage[:, 4 * lo : 4 * hi].rearrange("p (c i j) -> p c j i", i=4, j=4),
-                x_raw[:, :, lo:hi].rearrange("p j (c i) -> p c j i", i=4),
+                x_stage[:, 4 * lo : 4 * hi].rearrange("p (c i j) -> p c j i", i=2, j=4),
+                x_raw[:, :, lo:hi].rearrange("p j (c i) -> p c j i", i=2),
             )
             quantize(x_codes[:, lo:hi], x_scales[:, lo:hi], x_stage[:, 4 * lo : 4 * hi])
 
@@ -120,14 +120,18 @@ def tile_moe_two_mlp_silu_kernel(tc, xT, w1, w2, gate, offs, dst, out):
 
         def copy_w1(e, s, m_vector):
             stage = ring.tile([P, 4 * HALF], BF16, name="w1_stage", align_bytes=64, bufs=4)
-            to = stage[:].rearrange("p (t m j) -> p m j t", t=4, j=4)
-            source = w1_raw[e][:, :, s * HALF : (s + 1) * HALF].rearrange("p j (m t) -> p m j t", t=4)
-            vcopy(to[:, :m_vector], source[:, :m_vector])
-            scopy(to[:, m_vector:], source[:, m_vector:])
+            to = stage[:].rearrange("p (u v m j) -> p u m j v", u=2, v=2, j=4)
+            source = w1_raw[e][:, :, s * HALF : (s + 1) * HALF].rearrange("p j (m u v) -> p u m j v", u=2, v=2)
+            vcopy(to[:, :, :m_vector], source[:, :, :m_vector])
+            scopy(to[:, :, m_vector:], source[:, :, m_vector:])
             return stage
 
         def first_layer(e, stage, s):
-            codes, scales = quantized("w1", stage[:], HALF)
+            codes, scales = new_operand("w1", HALF)
+            pieces = 2 if (e >= EARLY and s == HALVES - 1) else 1
+            words = HALF // pieces
+            for lo in range(0, HALF, words):
+                quantize(codes[:, lo : lo + words], scales[:, lo : lo + words], stage[:, 4 * lo : 4 * (lo + words)])
             slots = slice(e * C, (e + 1) * C)
             acc = psum_h.tile([P, 4, C], F32, name="acc_h")
             for t in range(4):
@@ -149,8 +153,8 @@ def tile_moe_two_mlp_silu_kernel(tc, xT, w1, w2, gate, offs, dst, out):
         def copy_w2(e, shares):
             staged = ring.tile([P, HALVES * 4 * N], BF16, name="w2_stage", align_bytes=64)
             stage = staged[:]
-            to = stage.rearrange("p (s c i j) -> p s c j i", s=HALVES, i=4, j=4)
-            source = w2_raw[e][:].rearrange("p s j (c i) -> p s c j i", i=4)
+            to = stage.rearrange("p (s c i j) -> p s c j i", s=HALVES, i=2, j=4)
+            source = w2_raw[e][:].rearrange("p s j (c i) -> p s c j i", i=2)
             for copy, passes in shares:
                 copy(to[:, passes], source[:, passes])
             return stage
@@ -195,8 +199,12 @@ def tile_moe_two_mlp_silu_kernel(tc, xT, w1, w2, gate, offs, dst, out):
             h = ring.tile([P, HALVES * 4 * C], BF16, name="h_stage", align_bytes=64)
             for s in range(HALVES):
                 apply_silu(accs[s], h[:, 4 * C * s : 4 * C * (s + 1)])
-            if e < last:
+            if e < EARLY:
                 h_q[e] = quantized("h", h[:], HALVES * C)
+            elif e < last:
+                h_q[e] = new_operand("h", HALVES * C)
+                for s in range(HALVES):
+                    quantize(h_q[e][0][:, C * s : C * (s + 1)], h_q[e][1][:, C * s : C * (s + 1)], h[:, 4 * C * s : 4 * C * (s + 1)])
             if e < EARLY:
                 acc_y = second_layer(w2_q[e], h_q[e])
         codes, scales = new_operand("h", HALVES * C)

@@ -74,10 +74,6 @@ def tile_moe_two_mlp_silu_kernel(tc, xT, w1, w2, gate, offs, dst, out):
         nc.gpsimd.memset(x_scales[:], 0)
         make_identity(nc, ident[:])
 
-        warm = keep.tile([P, 1], F32, name="warm")
-        nc.vector.memset(warm[:], 0.0)
-        nc.scalar.activation(warm[:], warm[:], SILU)
-
         def vcopy(dst_ap, src_ap):
             nc.vector.tensor_copy(dst_ap, src_ap)
 

@@ -53,7 +53,7 @@ def tile_moe_two_mlp_silu_kernel(tc, xT, w1, w2, gate, offs, dst, out):
         def load_w2(e):
             nc.sync.dma_start(w2_raw[e][:], w2[e].rearrange("(s p j) n -> p s j n", s=HALVES, j=4))
 
-        nc.sync.dma_start(gate_row[:], gate[0:1, :].rearrange("o (p m) -> (o p) m", m=GATES))
+        nc.scalar.dma_start(gate_row[:], gate[0:1, :].rearrange("o (p m) -> (o p) m", m=GATES))
         nc.sync.dma_start(x_raw[:], xT.rearrange("(p j) t -> p j t", j=4))
         nc.sync.dma_start(offs_sb[:], offs)
         for e in range(E):
@@ -124,7 +124,7 @@ def tile_moe_two_mlp_silu_kernel(tc, xT, w1, w2, gate, offs, dst, out):
 
         def first_layer(e, stage, s):
             codes, scales = new_operand("w1", HALF)
-            pieces = 2 if (e >= EARLY and s == HALVES - 1) else 1
+            pieces = 2 if (e == E - 1 or (e >= EARLY and s == HALVES - 1)) else 1
             words = HALF // pieces
             for lo in range(0, HALF, words):
                 quantize(codes[:, lo : lo + words], scales[:, lo : lo + words], stage[:, 4 * lo : 4 * (lo + words)])
@@ -203,6 +203,18 @@ def tile_moe_two_mlp_silu_kernel(tc, xT, w1, w2, gate, offs, dst, out):
                     quantize(h_q[e][0][:, C * s : C * (s + 1)], h_q[e][1][:, C * s : C * (s + 1)], h[:, 4 * C * s : 4 * C * (s + 1)])
             if e < EARLY:
                 acc_y = second_layer(w2_q[e], h_q[e])
+            if e == last - 1:
+                unread = psum_g.tile([P, 512], F32, name="spread")
+                for warm_up in range(3):
+                    nc.tensor.matmul_mx(
+                        out=unread[:],
+                        lhsT=h_q[e][0][:, :C].bitcast(FP8X4),
+                        lhsT_scale=h_q[e][1][:, :C],
+                        rhs=slot_codes[:, :512].bitcast(FP8X4),
+                        rhs_scale=slot_scales[:, :512],
+                        start=True,
+                        stop=True,
+                    )
         codes, scales = new_operand("h", HALVES * C)
         quantize(codes[:, :C], scales[:, :C], h[:, : 4 * C])
         y = times_gate(last - 1, acc_y, w1_raw[last])

@@ -24,6 +24,7 @@ X_VECTOR = 512
 GATHER = 384
 M_VECTOR = 80
 M_VECTOR_FIRST = 64
+M_VECTOR_LAST = 84
 GATES = T // P
 
 
@@ -181,7 +182,7 @@ def tile_moe_two_mlp_silu_kernel(tc, xT, w1, w2, gate, offs, dst, out):
         h_q, w2_q = {}, {}
         last = E - 1
         for e in range(E):
-            share = M_VECTOR if e > 0 else M_VECTOR_FIRST
+            share = M_VECTOR_LAST if e == last else M_VECTOR if e > 0 else M_VECTOR_FIRST
             stages = [copy_w1(e, s, share) for s in range(HALVES)]
             accs = [first_layer(e, stages[s], s) for s in range(HALVES)]
             if 0 < e <= EARLY:
@@ -189,8 +190,15 @@ def tile_moe_two_mlp_silu_kernel(tc, xT, w1, w2, gate, offs, dst, out):
             if e < EARLY:
                 w2_q[e] = quantized("w2", copy_w2(e, [(scopy, slice(0, 2))]), HALVES * N)
             if e == last:
-                w2_q[e - 1] = quantized("w2", copy_w2(e - 1, [(scopy, slice(0, 2))]), HALVES * N)
-                w2_q[e] = quantized("w2", copy_w2(e, [(vcopy, slice(0, 2))]), HALVES * N)
+                stage4 = copy_w2(e - 1, [(scopy, slice(0, 1)), (scopy, slice(1, 2))])
+                w2_q[e - 1] = new_operand("w2", HALVES * N)
+                staged5 = ring.tile([P, HALVES * 4 * N], BF16, name="w2_stage", align_bytes=64)
+                to = staged5[:].rearrange("p (s c i j) -> p s c j i", s=HALVES, i=2, j=4)
+                source = w2_raw[e][:].rearrange("p s j (c i) -> p s c j i", i=2)
+                for s in range(HALVES):
+                    words = slice(N * s, N * (s + 1))
+                    quantize(w2_q[e - 1][0][:, words], w2_q[e - 1][1][:, words], stage4[:, 4 * N * s : 4 * N * (s + 1)])
+                    vcopy(to[:, s : s + 1], source[:, s : s + 1])
                 acc_y = second_layer(w2_q[e - 1], h_q[e - 1])
             h = ring.tile([P, HALVES * 4 * C], BF16, name="h_stage", align_bytes=64)
             for s in range(HALVES):
@@ -217,6 +225,7 @@ def tile_moe_two_mlp_silu_kernel(tc, xT, w1, w2, gate, offs, dst, out):
                     )
         codes, scales = new_operand("h", HALVES * C)
         quantize(codes[:, :C], scales[:, :C], h[:, : 4 * C])
+        w2_q[last] = quantized("w2", staged5[:], HALVES * N)
         y = times_gate(last - 1, acc_y, w1_raw[last])
         quantize(codes[:, C:], scales[:, C:], h[:, 4 * C :])
         scatter(last - 1, y)

@@ -17,15 +17,17 @@ SILU = mybir.ActivationFunctionType.Silu
 MULT = mybir.AluOpType.mult
 
 P = 128
-EARLY = 4
+LAST = E - 1
+EARLY = E - 2
 HALF = 512
 HALVES = H // HALF
 X_VECTOR = 512
-GATHER = 384
+GATHER = T // 2
+GATES = T // P
 M_VECTOR = 80
 M_VECTOR_FIRST = 64
 M_VECTOR_LAST = 84
-GATES = T // P
+WARM_UPS = 3
 
 
 def tile_moe_two_mlp_silu_kernel(tc, xT, w1, w2, gate, offs, dst, out):
@@ -48,9 +50,6 @@ def tile_moe_two_mlp_silu_kernel(tc, xT, w1, w2, gate, offs, dst, out):
         gate_row = keep.tile([P, GATES], F32, name="gate_row")
         gate_sb = keep.tile([P, T], F32, name="gate_sb")
 
-        def load_w1(e):
-            nc.sync.dma_start(w1_raw[e][:], w1[e].rearrange("(p j) c -> p j c", j=4))
-
         def load_w2(e):
             nc.sync.dma_start(w2_raw[e][:], w2[e].rearrange("(s p j) n -> p s j n", s=HALVES, j=4))
 
@@ -58,7 +57,7 @@ def tile_moe_two_mlp_silu_kernel(tc, xT, w1, w2, gate, offs, dst, out):
         nc.sync.dma_start(x_raw[:], xT.rearrange("(p j) t -> p j t", j=4))
         nc.sync.dma_start(offs_sb[:], offs)
         for e in range(E):
-            load_w1(e)
+            nc.sync.dma_start(w1_raw[e][:], w1[e].rearrange("(p j) c -> p j c", j=4))
             if e == 0:
                 nc.sync.dma_start(dst_sb[:], dst)
             if e < EARLY:
@@ -75,20 +74,35 @@ def tile_moe_two_mlp_silu_kernel(tc, xT, w1, w2, gate, offs, dst, out):
         nc.gpsimd.memset(x_scales[:], 0)
         make_identity(nc, ident[:])
 
-        def vcopy(dst_ap, src_ap):
-            nc.vector.tensor_copy(dst_ap, src_ap)
+        def vcopy(to, source):
+            nc.vector.tensor_copy(to, source)
 
-        def scopy(dst_ap, src_ap):
-            nc.scalar.copy(dst_ap, src_ap)
+        def scopy(to, source):
+            nc.scalar.copy(to, source)
 
-        def quantize(codes, scales, stage):
-            nc.vector.quantize_mx(out=codes.bitcast(FP8X4), scales=scales, in_=stage)
+        def quantize(operand, stage, lo, hi):
+            codes, scales = operand
+            nc.vector.quantize_mx(
+                out=codes[:, lo:hi].bitcast(FP8X4), scales=scales[:, lo:hi], in_=stage[:, 4 * lo : 4 * hi]
+            )
 
-        for copy, lo in ((scopy, 0), (scopy, 3)):
+        def matmul(acc, stationary, moving, start, stop):
+            (w_codes, w_scales, w_lo), (a_codes, a_scales, a_lo) = stationary, moving
+            nc.tensor.matmul_mx(
+                out=acc,
+                lhsT=w_codes[:, w_lo : w_lo + P].bitcast(FP8X4),
+                lhsT_scale=w_scales[:, w_lo : w_lo + P],
+                rhs=a_codes[:, a_lo : a_lo + C].bitcast(FP8X4),
+                rhs_scale=a_scales[:, a_lo : a_lo + C],
+                start=start,
+                stop=stop,
+            )
+
+        for lo in range(0, GATES, 3):
             spread = psum_g.tile([P, 3, P], F32, name="spread")
             for m in range(3):
                 nc.tensor.transpose(spread[:, m, :], gate_row[:, lo + m : lo + m + 1].to_broadcast([P, P]), ident[:])
-            copy(
+            scopy(
                 gate_sb[:].rearrange("p (n m) -> p n m", m=GATES)[:, :, lo : lo + 3],
                 spread[:].rearrange("p m n -> p n m"),
             )
@@ -98,80 +112,63 @@ def tile_moe_two_mlp_silu_kernel(tc, xT, w1, w2, gate, offs, dst, out):
                 x_stage[:, 4 * lo : 4 * hi].rearrange("p (c i j) -> p c j i", i=2, j=4),
                 x_raw[:, :, lo:hi].rearrange("p j (c i) -> p c j i", i=2),
             )
-            quantize(x_codes[:, lo:hi], x_scales[:, lo:hi], x_stage[:, 4 * lo : 4 * hi])
+            quantize((x_codes, x_scales), x_stage, lo, hi)
 
         for lo in range(0, T, GATHER):
             picked = offs_sb[:, lo // 16 : (lo + GATHER) // 16]
             nc.vector.tensor_copy(slot_codes[:, lo : lo + GATHER], x_codes[:].indirect(picked))
             nc.vector.tensor_copy(slot_scales[:, lo : lo + GATHER], x_scales[:].indirect(picked))
 
-        def new_operand(name, words):
-            codes = ring.tile([P, words], U32, name=f"{name}_codes", align_bytes=64)
-            scales = ring.tile([P, words], U8, name=f"{name}_scales", align_bytes=64)
+        def new_operand(name, columns):
+            codes = ring.tile([P, columns], U32, name=f"{name}_codes", align_bytes=64)
+            scales = ring.tile([P, columns], U8, name=f"{name}_scales", align_bytes=64)
             return codes, scales
 
-        def quantized(name, stage, words):
-            codes, scales = new_operand(name, words)
-            quantize(codes[:], scales[:], stage)
-            return codes, scales
+        def stage_tag(e, s):
+            return f"w1_stage{e}_{s}"
 
-        def copy_w1(e, s, m_vector):
-            stage = ring.tile([P, 4 * HALF], BF16, name="w1_stage", align_bytes=64, bufs=4)
+        def interleave_w1(e, s, m_vector):
+            stage = keep.tile([P, 4 * HALF], BF16, name="w1_stage", tag=stage_tag(e, s), align_bytes=64)
             to = stage[:].rearrange("p (u v m j) -> p u m j v", u=2, v=2, j=4)
             source = w1_raw[e][:, :, s * HALF : (s + 1) * HALF].rearrange("p j (m u v) -> p u m j v", u=2, v=2)
             vcopy(to[:, :, :m_vector], source[:, :, :m_vector])
             scopy(to[:, :, m_vector:], source[:, :, m_vector:])
             return stage
 
-        def first_layer(e, stage, s):
-            codes, scales = new_operand("w1", HALF)
-            pieces = 2 if (e == E - 1 or (e >= EARLY and s == HALVES - 1)) else 1
-            words = HALF // pieces
-            for lo in range(0, HALF, words):
-                quantize(codes[:, lo : lo + words], scales[:, lo : lo + words], stage[:, 4 * lo : 4 * (lo + words)])
-            slots = slice(e * C, (e + 1) * C)
+        def first_layer(e, stage):
+            columns = HALF // 2 if e >= EARLY else HALF
+            w1_q = new_operand("w1", HALF)
+            for lo in range(0, HALF, columns):
+                quantize(w1_q, stage, lo, lo + columns)
             acc = psum_h.tile([P, 4, C], F32, name="acc_h")
             for t in range(4):
-                cols = slice(128 * t, 128 * (t + 1))
-                nc.tensor.matmul_mx(
-                    out=acc[:, t, :],
-                    lhsT=codes[:, cols].bitcast(FP8X4),
-                    lhsT_scale=scales[:, cols],
-                    rhs=slot_codes[:, slots].bitcast(FP8X4),
-                    rhs_scale=slot_scales[:, slots],
-                    start=True,
-                    stop=True,
-                )
+                matmul(acc[:, t, :], (*w1_q, P * t), (slot_codes, slot_scales, C * e), True, True)
             return acc
 
-        def apply_silu(acc, h):
-            nc.scalar.activation(h.rearrange("p (n t) -> p n t", t=4), acc[:].rearrange("p t n -> p n t"), SILU)
+        def silu(accs):
+            h = ring.tile([P, HALVES * 4 * C], BF16, name="h_stage", align_bytes=64)
+            for s, acc in enumerate(accs):
+                to = h[:, 4 * C * s : 4 * C * (s + 1)].rearrange("p (n t) -> p n t", t=4)
+                nc.scalar.activation(to, acc[:].rearrange("p t n -> p n t"), SILU)
+            return h
 
-        def copy_w2(e, shares):
-            staged = ring.tile([P, HALVES * 4 * N], BF16, name="w2_stage", align_bytes=64)
-            stage = staged[:]
-            to = stage.rearrange("p (s c i j) -> p s c j i", s=HALVES, i=2, j=4)
-            source = w2_raw[e][:].rearrange("p s j (c i) -> p s c j i", i=2)
-            for copy, passes in shares:
-                copy(to[:, passes], source[:, passes])
+        def new_w2_stage():
+            stage = ring.tile([P, HALVES * 4 * N], BF16, name="w2_stage", align_bytes=64)
             return stage
 
-        def second_layer(w2_q, h_q):
+        def interleave_w2(copy, e, stage, first, stop):
+            to = stage[:].rearrange("p (s c i j) -> p s c j i", s=HALVES, i=2, j=4)
+            source = w2_raw[e][:].rearrange("p s j (c i) -> p s c j i", i=2)
+            copy(to[:, first:stop], source[:, first:stop])
+
+        def second_layer(w2_q, h_passes):
             acc = psum_y.tile([P, C], F32, name="acc_y")
             for s in range(HALVES):
-                nc.tensor.matmul_mx(
-                    out=acc[:],
-                    lhsT=w2_q[0][:, N * s : N * (s + 1)].bitcast(FP8X4),
-                    lhsT_scale=w2_q[1][:, N * s : N * (s + 1)],
-                    rhs=h_q[0][:, C * s : C * (s + 1)].bitcast(FP8X4),
-                    rhs_scale=h_q[1][:, C * s : C * (s + 1)],
-                    start=(s == 0),
-                    stop=(s == HALVES - 1),
-                )
+                matmul(acc[:], (*w2_q, N * s), h_passes[s], s == 0, s == HALVES - 1)
             return acc
 
-        def times_gate(e, acc, over):
-            y = over[:, 2, HALF : HALF + C]
+        def times_gate(e, acc, spent):
+            y = spent[:, 2, HALF : HALF + C]
             nc.vector.tensor_tensor(y, acc[:], gate_sb[:, e * C : (e + 1) * C], MULT)
             return y
 
@@ -179,56 +176,58 @@ def tile_moe_two_mlp_silu_kernel(tc, xT, w1, w2, gate, offs, dst, out):
             places = dst_sb[:, e * C // 16 : (e + 1) * C // 16]
             nc.vector.tensor_copy(out_sb[:].indirect(places), y)
 
-        h_q, w2_q = {}, {}
-        last = E - 1
-        for e in range(E):
-            share = M_VECTOR_LAST if e == last else M_VECTOR if e > 0 else M_VECTOR_FIRST
-            stages = [copy_w1(e, s, share) for s in range(HALVES)]
-            accs = [first_layer(e, stages[s], s) for s in range(HALVES)]
-            if 0 < e <= EARLY:
+        def first_layers(e, m_vector):
+            stages = [interleave_w1(e, s, m_vector) for s in range(HALVES)]
+            return [first_layer(e, stage) for stage in stages]
+
+        for e in range(EARLY):
+            accs = first_layers(e, M_VECTOR if e > 0 else M_VECTOR_FIRST)
+            if e > 0:
                 scatter(e - 1, times_gate(e - 1, acc_y, w1_raw[e]))
-            if e < EARLY:
-                w2_q[e] = quantized("w2", copy_w2(e, [(scopy, slice(0, 2))]), HALVES * N)
-            if e == last:
-                stage4 = copy_w2(e - 1, [(scopy, slice(0, 1)), (scopy, slice(1, 2))])
-                w2_q[e - 1] = new_operand("w2", HALVES * N)
-                staged5 = ring.tile([P, HALVES * 4 * N], BF16, name="w2_stage", align_bytes=64)
-                to = staged5[:].rearrange("p (s c i j) -> p s c j i", s=HALVES, i=2, j=4)
-                source = w2_raw[e][:].rearrange("p s j (c i) -> p s c j i", i=2)
-                for s in range(HALVES):
-                    words = slice(N * s, N * (s + 1))
-                    quantize(w2_q[e - 1][0][:, words], w2_q[e - 1][1][:, words], stage4[:, 4 * N * s : 4 * N * (s + 1)])
-                    vcopy(to[:, s : s + 1], source[:, s : s + 1])
-                acc_y = second_layer(w2_q[e - 1], h_q[e - 1])
-            h = ring.tile([P, HALVES * 4 * C], BF16, name="h_stage", align_bytes=64)
-            for s in range(HALVES):
-                apply_silu(accs[s], h[:, 4 * C * s : 4 * C * (s + 1)])
-            if e < EARLY:
-                h_q[e] = quantized("h", h[:], HALVES * C)
-            elif e < last:
-                h_q[e] = new_operand("h", HALVES * C)
-                for s in range(HALVES):
-                    quantize(h_q[e][0][:, C * s : C * (s + 1)], h_q[e][1][:, C * s : C * (s + 1)], h[:, 4 * C * s : 4 * C * (s + 1)])
-            if e < EARLY:
-                acc_y = second_layer(w2_q[e], h_q[e])
-            if e == last - 1:
-                unread = psum_g.tile([P, 512], F32, name="spread")
-                for warm_up in range(3):
-                    nc.tensor.matmul_mx(
-                        out=unread[:],
-                        lhsT=h_q[e][0][:, :C].bitcast(FP8X4),
-                        lhsT_scale=h_q[e][1][:, :C],
-                        rhs=slot_codes[:, :512].bitcast(FP8X4),
-                        rhs_scale=slot_scales[:, :512],
-                        start=True,
-                        stop=True,
-                    )
-        codes, scales = new_operand("h", HALVES * C)
-        quantize(codes[:, :C], scales[:, :C], h[:, : 4 * C])
-        w2_q[last] = quantized("w2", staged5[:], HALVES * N)
-        y = times_gate(last - 1, acc_y, w1_raw[last])
-        quantize(codes[:, C:], scales[:, C:], h[:, 4 * C :])
-        scatter(last - 1, y)
-        acc_y = second_layer(w2_q[last], (codes, scales))
-        scatter(last, times_gate(last, acc_y, w1_raw[0]))
+            w2_stage, w2_q = new_w2_stage(), new_operand("w2", HALVES * N)
+            interleave_w2(scopy, e, w2_stage, 0, HALVES)
+            quantize(w2_q, w2_stage, 0, HALVES * N)
+            h, h_q = silu(accs), new_operand("h", HALVES * C)
+            quantize(h_q, h, 0, HALVES * C)
+            acc_y = second_layer(w2_q, [(*h_q, C * s) for s in range(HALVES)])
+
+        accs = first_layers(EARLY, M_VECTOR)
+        scatter(EARLY - 1, times_gate(EARLY - 1, acc_y, w1_raw[EARLY]))
+        h_before, h_before_q0 = silu(accs), new_operand("h", HALVES * C)
+        quantize(h_before_q0, h_before, 0, C)
+
+        unread = psum_g.tile([P, HALF], F32, name="spread")
+        for warm_up in range(WARM_UPS):
+            nc.tensor.matmul_mx(
+                out=unread[:],
+                lhsT=h_before_q0[0][:, :P].bitcast(FP8X4),
+                lhsT_scale=h_before_q0[1][:, :P],
+                rhs=slot_codes[:, :HALF].bitcast(FP8X4),
+                rhs_scale=slot_scales[:, :HALF],
+                start=True,
+                stop=True,
+            )
+
+        accs = first_layers(LAST, M_VECTOR_LAST)
+        late_codes = keep.tile([P, HALVES * C], U32, name="late_codes", tag=stage_tag(LAST, 1), align_bytes=64)
+        h_before_q1 = (late_codes, h_before_q0[1])
+        quantize(h_before_q1, h_before, C, 2 * C)
+
+        w2_before, w2_before_q = new_w2_stage(), new_operand("w2", HALVES * N)
+        w2_last = new_w2_stage()
+        for s in range(HALVES):
+            interleave_w2(scopy, EARLY, w2_before, s, s + 1)
+        for s in range(HALVES):
+            quantize(w2_before_q, w2_before, N * s, N * (s + 1))
+            interleave_w2(vcopy, LAST, w2_last, s, s + 1)
+        acc_before = second_layer(w2_before_q, [(*h_before_q0, 0), (*h_before_q1, C)])
+
+        h, h_q, w2_q = silu(accs), new_operand("h", HALVES * C), new_operand("w2", HALVES * N)
+        quantize(h_q, h, 0, C)
+        quantize(w2_q, w2_last, 0, HALVES * N)
+        y_before = times_gate(EARLY, acc_before, w1_raw[LAST])
+        quantize(h_q, h, C, 2 * C)
+        scatter(EARLY, y_before)
+        acc_y = second_layer(w2_q, [(*h_q, C * s) for s in range(HALVES)])
+        scatter(LAST, times_gate(LAST, acc_y, w1_raw[0]))
         nc.sync.dma_start(out, out_sb[:])

@@ -27,7 +27,6 @@ GATES = T // P
 M_VECTOR = 80
 M_VECTOR_FIRST = 64
 M_VECTOR_LAST = 84
-WARM_UPS = 3
 
 
 def tile_moe_two_mlp_silu_kernel(tc, xT, w1, w2, gate, offs, dst, out):
@@ -195,19 +194,6 @@ def tile_moe_two_mlp_silu_kernel(tc, xT, w1, w2, gate, offs, dst, out):
         scatter(EARLY - 1, times_gate(EARLY - 1, acc_y, w1_raw[EARLY]))
         h_before, h_before_q0 = silu(accs), new_operand("h", HALVES * C)
         quantize(h_before_q0, h_before, 0, C)
-
-        unread = psum_g.tile([P, HALF], F32, name="spread")
-        for warm_up in range(WARM_UPS):
-            nc.tensor.matmul_mx(
-                out=unread[:],
-                lhsT=h_before_q0[0][:, :P].bitcast(FP8X4),
-                lhsT_scale=h_before_q0[1][:, :P],
-                rhs=slot_codes[:, :HALF].bitcast(FP8X4),
-                rhs_scale=slot_scales[:, :HALF],
-                start=True,
-                stop=True,
-            )
-
         accs = first_layers(LAST, M_VECTOR_LAST)
         late_codes = keep.tile([P, HALVES * C], U32, name="late_codes", tag=stage_tag(LAST, 1), align_bytes=64)
         h_before_q1 = (late_codes, h_before_q0[1])

@@ -175,6 +175,15 @@ def tile_moe_two_mlp_silu_kernel(tc, xT, w1, w2, gate, offs, dst, out):
             places = dst_sb[:, e * C // 16 : (e + 1) * C // 16]
             nc.vector.tensor_copy(out_sb[:].indirect(places), y)
 
+        def empty(acc):
+            y = ring.tile([P, C], F32, name="y")
+            scopy(y[:], acc[:])
+            return y
+
+        def scatter_times_gate(e, y):
+            places = dst_sb[:, e * C // 16 : (e + 1) * C // 16]
+            nc.vector.tensor_tensor(out_sb[:].indirect(places), y[:], gate_sb[:, e * C : (e + 1) * C], MULT)
+
         def first_layers(e, m_vector):
             stages = [interleave_w1(e, s, m_vector) for s in range(HALVES)]
             return [first_layer(e, stage) for stage in stages]
@@ -209,11 +218,10 @@ def tile_moe_two_mlp_silu_kernel(tc, xT, w1, w2, gate, offs, dst, out):
         acc_before = second_layer(w2_before_q, [(*h_before_q0, 0), (*h_before_q1, C)])
 
         h, h_q, w2_q = silu(accs), new_operand("h", HALVES * C), new_operand("w2", HALVES * N)
+        quantize(w2_q, w2_last, 0, N)
         quantize(h_q, h, 0, C)
-        quantize(w2_q, w2_last, 0, HALVES * N)
-        y_before = times_gate(EARLY, acc_before, w1_raw[LAST])
+        quantize(w2_q, w2_last, N, 2 * N)
         quantize(h_q, h, C, 2 * C)
-        scatter(EARLY, y_before)
-        acc_y = second_layer(w2_q, [(*h_q, C * s) for s in range(HALVES)])
-        scatter(LAST, times_gate(LAST, acc_y, w1_raw[0]))
+        scatter_times_gate(EARLY, empty(acc_before))
+        scatter_times_gate(LAST, empty(second_layer(w2_q, [(*h_q, C * s) for s in range(HALVES)])))
         nc.sync.dma_start(out, out_sb[:])

@@ -50,7 +50,12 @@ def tile_moe_two_mlp_silu_kernel(tc, xT, w1, w2, gate, offs, dst, out):
         gate_sb = keep.tile([P, T], F32, name="gate_sb")
 
         def load_w2(e):
-            nc.sync.dma_start(w2_raw[e][:], w2[e].rearrange("(s p j) n -> p s j n", s=HALVES, j=4))
+            rows = w2[e].rearrange("(s p j) n -> p s j n", s=HALVES, j=4)
+            if e < EARLY:
+                for s in range(HALVES):
+                    nc.sync.dma_start(w2_raw[e][:, s], rows[:, s])
+            else:
+                nc.sync.dma_start(w2_raw[e][:], rows)
 
         nc.scalar.dma_start(gate_row[:], gate[0:1, :].rearrange("o (p m) -> (o p) m", m=GATES))
         nc.sync.dma_start(x_raw[:], xT.rearrange("(p j) t -> p j t", j=4))

@@ -51,11 +51,8 @@ def tile_moe_two_mlp_silu_kernel(tc, xT, w1, w2, gate, offs, dst, out):
 
         def load_w2(e):
             rows = w2[e].rearrange("(s p j) n -> p s j n", s=HALVES, j=4)
-            if e < EARLY:
-                for s in range(HALVES):
-                    nc.sync.dma_start(w2_raw[e][:, s], rows[:, s])
-            else:
-                nc.sync.dma_start(w2_raw[e][:], rows)
+            for s in range(HALVES):
+                nc.sync.dma_start(w2_raw[e][:, s], rows[:, s])
 
         nc.scalar.dma_start(gate_row[:], gate[0:1, :].rearrange("o (p m) -> (o p) m", m=GATES))
         nc.sync.dma_start(x_raw[:], xT.rearrange("(p j) t -> p j t", j=4))

@@ -25,8 +25,9 @@ X_VECTOR = 512
 GATHER = T // 2
 GATES = T // P
 M_VECTOR = 80
+WHOLE, TWO, THREE = (0, HALF), (0, HALF // 2, HALF), (0, HALF // 2, 3 * HALF // 4, HALF)
 M_VECTOR_FIRST = 64
-M_VECTOR_LAST = 84
+M_VECTOR_LAST = 44
 
 
 def tile_moe_two_mlp_silu_kernel(tc, xT, w1, w2, gate, offs, dst, out):
@@ -132,15 +133,18 @@ def tile_moe_two_mlp_silu_kernel(tc, xT, w1, w2, gate, offs, dst, out):
             stage = keep.tile([P, 4 * HALF], BF16, name="w1_stage", tag=stage_tag(e, s), align_bytes=64)
             to = stage[:].rearrange("p (u v m j) -> p u m j v", u=2, v=2, j=4)
             source = w1_raw[e][:, :, s * HALF : (s + 1) * HALF].rearrange("p j (m u v) -> p u m j v", u=2, v=2)
-            vcopy(to[:, :, :m_vector], source[:, :, :m_vector])
-            scopy(to[:, :, m_vector:], source[:, :, m_vector:])
+            if m_vector < P:
+                vcopy(to[:, :, :m_vector], source[:, :, :m_vector])
+                scopy(to[:, :, m_vector:], source[:, :, m_vector:])
+            else:
+                for u in range(2):
+                    vcopy(to[:, u], source[:, u])
             return stage
 
-        def first_layer(e, stage):
-            columns = HALF // 2 if e >= EARLY else HALF
+        def first_layer(e, stage, cuts):
             w1_q = new_operand("w1", HALF)
-            for lo in range(0, HALF, columns):
-                quantize(w1_q, stage, lo, lo + columns)
+            for lo, hi in zip(cuts, cuts[1:]):
+                quantize(w1_q, stage, lo, hi)
             acc = psum_h.tile([P, 4, C], F32, name="acc_h")
             for t in range(4):
                 matmul(acc[:, t, :], (*w1_q, P * t), (slot_codes, slot_scales, C * e), True, True)
@@ -188,7 +192,7 @@ def tile_moe_two_mlp_silu_kernel(tc, xT, w1, w2, gate, offs, dst, out):
 
         def first_layers(e, m_vector):
             stages = [interleave_w1(e, s, m_vector) for s in range(HALVES)]
-            return [first_layer(e, stage) for stage in stages]
+            return [first_layer(e, stage, TWO if e >= EARLY else WHOLE) for stage in stages]
 
         for e in range(EARLY):
             accs = first_layers(e, M_VECTOR if e > 0 else M_VECTOR_FIRST)
@@ -205,7 +209,8 @@ def tile_moe_two_mlp_silu_kernel(tc, xT, w1, w2, gate, offs, dst, out):
         scatter(EARLY - 1, times_gate(EARLY - 1, acc_y, w1_raw[EARLY]))
         h_before, h_before_q0 = silu(accs), new_operand("h", HALVES * C)
         quantize(h_before_q0, h_before, 0, C)
-        accs = first_layers(LAST, M_VECTOR_LAST)
+        stages = [interleave_w1(LAST, 0, P), interleave_w1(LAST, 1, M_VECTOR_LAST)]
+        accs = [first_layer(LAST, stages[0], TWO), first_layer(LAST, stages[1], THREE)]
         late_codes = keep.tile([P, HALVES * C], U32, name="late_codes", tag=stage_tag(LAST, 1), align_bytes=64)
         h_before_q1 = (late_codes, h_before_q0[1])
         quantize(h_before_q1, h_before, C, 2 * C)
@@ -216,6 +221,7 @@ def tile_moe_two_mlp_silu_kernel(tc, xT, w1, w2, gate, offs, dst, out):
             interleave_w2(scopy, EARLY, w2_before, s, s + 1)
         for s in range(HALVES):
             quantize(w2_before_q, w2_before, N * s, N * (s + 1))
+        for s in range(HALVES):
             interleave_w2(vcopy, LAST, w2_last, s, s + 1)
         acc_before = second_layer(w2_before_q, [(*h_before_q0, 0), (*h_before_q1, C)])
 

@@ -26,7 +26,6 @@ GATHER = T // 2
 GATES = T // P
 M_VECTOR = 80
 WHOLE, TWO, THREE = (0, HALF), (0, HALF // 2, HALF), (0, HALF // 2, 3 * HALF // 4, HALF)
-M_VECTOR_FIRST = 64
 M_VECTOR_LAST = 44
 
 
@@ -44,7 +43,7 @@ def tile_moe_two_mlp_silu_kernel(tc, xT, w1, w2, gate, offs, dst, out):
         dst_sb = lists.tile([P, T // 16], U16, name="dst_sb")
 
         x_raw = keep.tile([P, 4, T], F32, name="x_raw")
-        w1_raw = [keep.tile([P, 4, H], F32, name=f"w1_raw{e}") for e in range(E)]
+        w1_raw = [keep.tile([P, 4, H], F32, name=f"w1_raw{e}", align_bytes=64) for e in range(E)]
         w2_raw = [keep.tile([P, HALVES, 4, N], F32, name=f"w2_raw{e}", align_bytes=64) for e in range(E)]
         x_stage = keep.tile([P, 4 * T], BF16, name="x_stage", align_bytes=64)
         gate_row = keep.tile([P, GATES], F32, name="gate_row")
@@ -69,8 +68,6 @@ def tile_moe_two_mlp_silu_kernel(tc, xT, w1, w2, gate, offs, dst, out):
 
         x_codes = keep.tile([P, T], U32, name="x_codes", align_bytes=64)
         x_scales = keep.tile([P, T], U8, name="x_scales", align_bytes=64)
-        slot_codes = keep.tile([P, T], U32, name="slot_codes", align_bytes=64)
-        slot_scales = keep.tile([P, T], U8, name="slot_scales", align_bytes=64)
         out_sb = keep.tile([P, T], F32, name="out_sb")
         ident = keep.tile([P, P], F32, name="ident")
         nc.gpsimd.memset(x_scales[:], 0)
@@ -116,10 +113,15 @@ def tile_moe_two_mlp_silu_kernel(tc, xT, w1, w2, gate, offs, dst, out):
             )
             quantize((x_codes, x_scales), x_stage, lo, hi)
 
-        for lo in range(0, T, GATHER):
-            picked = offs_sb[:, lo // 16 : (lo + GATHER) // 16]
-            nc.vector.tensor_copy(slot_codes[:, lo : lo + GATHER], x_codes[:].indirect(picked))
-            nc.vector.tensor_copy(slot_scales[:, lo : lo + GATHER], x_scales[:].indirect(picked))
+        def gather(part, codes_tag, scales_tag):
+            codes = keep.tile([P, GATHER], U32, name="slot_codes", tag=codes_tag, align_bytes=64)
+            scales = keep.tile([P, GATHER], U8, name="slot_scales", tag=scales_tag, align_bytes=64)
+            picked = offs_sb[:, part * GATHER // 16 : (part + 1) * GATHER // 16]
+            nc.vector.tensor_copy(codes[:], x_codes[:].indirect(picked))
+            nc.vector.tensor_copy(scales[:], x_scales[:].indirect(picked))
+            return codes, scales
+
+        slots = [gather(0, "slot_codes", "slot_scales")]
 
         def new_operand(name, columns):
             codes = ring.tile([P, columns], U32, name=f"{name}_codes", align_bytes=64)
@@ -147,7 +149,7 @@ def tile_moe_two_mlp_silu_kernel(tc, xT, w1, w2, gate, offs, dst, out):
                 quantize(w1_q, stage, lo, hi)
             acc = psum_h.tile([P, 4, C], F32, name="acc_h")
             for t in range(4):
-                matmul(acc[:, t, :], (*w1_q, P * t), (slot_codes, slot_scales, C * e), True, True)
+                matmul(acc[:, t, :], (*w1_q, P * t), (*slots[C * e // GATHER], C * e % GATHER), True, True)
             return acc
 
         def silu(accs):
@@ -195,13 +197,19 @@ def tile_moe_two_mlp_silu_kernel(tc, xT, w1, w2, gate, offs, dst, out):
             return [first_layer(e, stage, TWO if e >= EARLY else WHOLE) for stage in stages]
 
         for e in range(EARLY):
-            accs = first_layers(e, M_VECTOR if e > 0 else M_VECTOR_FIRST)
+            accs = first_layers(e, M_VECTOR)
             if e > 0:
                 scatter(e - 1, times_gate(e - 1, acc_y, w1_raw[e]))
-            w2_stage, w2_q = new_w2_stage(), new_operand("w2", HALVES * N)
-            interleave_w2(scopy, e, w2_stage, 0, HALVES)
+                w2_stage = new_w2_stage()
+                interleave_w2(scopy, e, w2_stage, 0, HALVES)
+                h = silu(accs)
+            else:
+                slots.append(gather(1, stage_tag(0, 0), "w1_raw0"))
+                h = silu(accs)
+                w2_stage = keep.tile([P, HALVES * 4 * N], BF16, name="w2_first", tag=stage_tag(0, 1), align_bytes=64)
+                interleave_w2(scopy, e, w2_stage, 0, HALVES)
+            w2_q, h_q = new_operand("w2", HALVES * N), new_operand("h", HALVES * C)
             quantize(w2_q, w2_stage, 0, HALVES * N)
-            h, h_q = silu(accs), new_operand("h", HALVES * C)
             quantize(h_q, h, 0, HALVES * C)
             acc_y = second_layer(w2_q, [(*h_q, C * s) for s in range(HALVES)])
 

@@ -21,12 +21,11 @@ LAST = E - 1
 EARLY = E - 2
 HALF = 512
 HALVES = H // HALF
-X_VECTOR = 512
 GATHER = T // 2
 GATES = T // P
 M_VECTOR = 80
 WHOLE, TWO, THREE = (0, HALF), (0, HALF // 2, HALF), (0, HALF // 2, 3 * HALF // 4, HALF)
-M_VECTOR_LAST = 44
+M_VECTOR_LAST = 52
 
 
 def tile_moe_two_mlp_silu_kernel(tc, xT, w1, w2, gate, offs, dst, out):
@@ -58,7 +57,10 @@ def tile_moe_two_mlp_silu_kernel(tc, xT, w1, w2, gate, offs, dst, out):
         nc.sync.dma_start(x_raw[:], xT.rearrange("(p j) t -> p j t", j=4))
         nc.sync.dma_start(offs_sb[:], offs)
         for e in range(E):
-            nc.sync.dma_start(w1_raw[e][:], w1[e].rearrange("(p j) c -> p j c", j=4))
+            run, rows = w1_raw[e][:].rearrange("p j c -> p (j c)"), w1[e].rearrange("(p j) c -> p (j c)", j=4)
+            cuts = (0, 4 * H - HALF, 4 * H) if e == LAST else (0, 4 * H)
+            for lo, hi in zip(cuts, cuts[1:]):
+                nc.sync.dma_start(run[:, lo:hi], rows[:, lo:hi])
             if e == 0:
                 nc.sync.dma_start(dst_sb[:], dst)
             if e < EARLY:
@@ -106,22 +108,23 @@ def tile_moe_two_mlp_silu_kernel(tc, xT, w1, w2, gate, offs, dst, out):
                 spread[:].rearrange("p m n -> p n m"),
             )
 
-        for copy, lo, hi in ((vcopy, 0, X_VECTOR), (scopy, X_VECTOR, T)):
-            copy(
-                x_stage[:, 4 * lo : 4 * hi].rearrange("p (c i j) -> p c j i", i=2, j=4),
-                x_raw[:, :, lo:hi].rearrange("p j (c i) -> p c j i", i=2),
-            )
-            quantize((x_codes, x_scales), x_stage, lo, hi)
+        vcopy(
+            x_stage[:].rearrange("p (c i j) -> p c j i", i=2, j=4),
+            x_raw[:].rearrange("p j (c i) -> p c j i", i=2),
+        )
+        for lo in range(0, T, T // 2):
+            quantize((x_codes, x_scales), x_stage, lo, lo + T // 2)
 
-        def gather(part, codes_tag, scales_tag):
+        def gather(part, codes_tag, scales_tag, cuts):
             codes = keep.tile([P, GATHER], U32, name="slot_codes", tag=codes_tag, align_bytes=64)
             scales = keep.tile([P, GATHER], U8, name="slot_scales", tag=scales_tag, align_bytes=64)
-            picked = offs_sb[:, part * GATHER // 16 : (part + 1) * GATHER // 16]
-            nc.vector.tensor_copy(codes[:], x_codes[:].indirect(picked))
-            nc.vector.tensor_copy(scales[:], x_scales[:].indirect(picked))
+            for lo, hi in zip(cuts, cuts[1:]):
+                picked = offs_sb[:, (part * GATHER + lo) // 16 : (part * GATHER + hi) // 16]
+                nc.vector.tensor_copy(codes[:, lo:hi], x_codes[:].indirect(picked))
+                nc.vector.tensor_copy(scales[:, lo:hi], x_scales[:].indirect(picked))
             return codes, scales
 
-        slots = [gather(0, "slot_codes", "slot_scales")]
+        slots = [gather(0, "slot_codes", "slot_scales", (0, C, 3 * C))]
 
         def new_operand(name, columns):
             codes = ring.tile([P, columns], U32, name=f"{name}_codes", align_bytes=64)
@@ -138,9 +141,11 @@ def tile_moe_two_mlp_silu_kernel(tc, xT, w1, w2, gate, offs, dst, out):
             if m_vector < P:
                 vcopy(to[:, :, :m_vector], source[:, :, :m_vector])
                 scopy(to[:, :, m_vector:], source[:, :, m_vector:])
-            else:
+            elif e == LAST:
                 for u in range(2):
                     vcopy(to[:, u], source[:, u])
+            else:
+                vcopy(to, source)
             return stage
 
         def first_layer(e, stage, cuts):
@@ -186,25 +191,25 @@ def tile_moe_two_mlp_silu_kernel(tc, xT, w1, w2, gate, offs, dst, out):
         def empty(acc):
             y = ring.tile([P, C], F32, name="y")
             scopy(y[:], acc[:])
-            return y
+            return y[:]
 
         def scatter_times_gate(e, y):
             places = dst_sb[:, e * C // 16 : (e + 1) * C // 16]
-            nc.vector.tensor_tensor(out_sb[:].indirect(places), y[:], gate_sb[:, e * C : (e + 1) * C], MULT)
+            nc.vector.tensor_tensor(out_sb[:].indirect(places), y, gate_sb[:, e * C : (e + 1) * C], MULT)
 
         def first_layers(e, m_vector):
-            stages = [interleave_w1(e, s, m_vector) for s in range(HALVES)]
-            return [first_layer(e, stage, TWO if e >= EARLY else WHOLE) for stage in stages]
+            stages = [interleave_w1(e, s, m_vector[s]) for s in range(HALVES)]
+            return [first_layer(e, stage, TWO if e + s >= EARLY else WHOLE) for s, stage in enumerate(stages)]
 
         for e in range(EARLY):
-            accs = first_layers(e, M_VECTOR)
+            accs = first_layers(e, (P, 2 * M_VECTOR - P) if e < 2 else (M_VECTOR, M_VECTOR))
             if e > 0:
                 scatter(e - 1, times_gate(e - 1, acc_y, w1_raw[e]))
                 w2_stage = new_w2_stage()
                 interleave_w2(scopy, e, w2_stage, 0, HALVES)
                 h = silu(accs)
             else:
-                slots.append(gather(1, stage_tag(0, 0), "w1_raw0"))
+                slots.append(gather(1, stage_tag(0, 0), "w1_raw0", (0, C, 3 * C)))
                 h = silu(accs)
                 w2_stage = keep.tile([P, HALVES * 4 * N], BF16, name="w2_first", tag=stage_tag(0, 1), align_bytes=64)
                 interleave_w2(scopy, e, w2_stage, 0, HALVES)
@@ -213,25 +218,27 @@ def tile_moe_two_mlp_silu_kernel(tc, xT, w1, w2, gate, offs, dst, out):
             quantize(h_q, h, 0, HALVES * C)
             acc_y = second_layer(w2_q, [(*h_q, C * s) for s in range(HALVES)])
 
-        accs = first_layers(EARLY, M_VECTOR)
-        scatter(EARLY - 1, times_gate(EARLY - 1, acc_y, w1_raw[EARLY]))
-        h_before, h_before_q0 = silu(accs), new_operand("h", HALVES * C)
-        quantize(h_before_q0, h_before, 0, C)
+        accs = first_layers(EARLY, (M_VECTOR, M_VECTOR))
+        y = w1_raw[EARLY][:, 3, H - C :]
+        scopy(y, acc_y[:])
+        scatter_times_gate(EARLY - 1, y)
+        h_before = silu(accs)
         stages = [interleave_w1(LAST, 0, P), interleave_w1(LAST, 1, M_VECTOR_LAST)]
         accs = [first_layer(LAST, stages[0], TWO), first_layer(LAST, stages[1], THREE)]
         late_codes = keep.tile([P, HALVES * C], U32, name="late_codes", tag=stage_tag(LAST, 1), align_bytes=64)
-        h_before_q1 = (late_codes, h_before_q0[1])
-        quantize(h_before_q1, h_before, C, 2 * C)
+        late_scales = keep.tile([P, HALVES * C], U8, name="late_scales", align_bytes=64)
+        h_before_q = (late_codes, late_scales)
 
         w2_before, w2_before_q = new_w2_stage(), new_operand("w2", HALVES * N)
         w2_last = new_w2_stage()
         for s in range(HALVES):
             interleave_w2(scopy, EARLY, w2_before, s, s + 1)
-        for s in range(HALVES):
-            quantize(w2_before_q, w2_before, N * s, N * (s + 1))
+        quantize(w2_before_q, w2_before, 0, N)
+        quantize(h_before_q, h_before, 0, HALVES * C)
+        quantize(w2_before_q, w2_before, N, 2 * N)
         for s in range(HALVES):
             interleave_w2(vcopy, LAST, w2_last, s, s + 1)
-        acc_before = second_layer(w2_before_q, [(*h_before_q0, 0), (*h_before_q1, C)])
+        acc_before = second_layer(w2_before_q, [(*h_before_q, C * s) for s in range(HALVES)])
 
         h, h_q, w2_q = silu(accs), new_operand("h", HALVES * C), new_operand("w2", HALVES * N)
         quantize(w2_q, w2_last, 0, N)

@@ -50,8 +50,11 @@ def tile_moe_two_mlp_silu_kernel(tc, xT, w1, w2, gate, offs, dst, out):
 
         def load_w2(e):
             rows = w2[e].rearrange("(s p j) n -> p s j n", s=HALVES, j=4)
-            for s in range(HALVES):
-                nc.sync.dma_start(w2_raw[e][:, s], rows[:, s])
+            if e == 0:
+                nc.sync.dma_start(w2_raw[e][:], rows)
+            else:
+                for s in range(HALVES):
+                    nc.sync.dma_start(w2_raw[e][:, s], rows[:, s])
 
         nc.scalar.dma_start(gate_row[:], gate[0:1, :].rearrange("o (p m) -> (o p) m", m=GATES))
         nc.sync.dma_start(x_raw[:], xT.rearrange("(p j) t -> p j t", j=4))
@@ -115,16 +118,15 @@ def tile_moe_two_mlp_silu_kernel(tc, xT, w1, w2, gate, offs, dst, out):
         for lo in range(0, T, T // 2):
             quantize((x_codes, x_scales), x_stage, lo, lo + T // 2)
 
-        def gather(part, codes_tag, scales_tag, cuts):
+        def gather(part, codes_tag, scales_tag):
             codes = keep.tile([P, GATHER], U32, name="slot_codes", tag=codes_tag, align_bytes=64)
             scales = keep.tile([P, GATHER], U8, name="slot_scales", tag=scales_tag, align_bytes=64)
-            for lo, hi in zip(cuts, cuts[1:]):
-                picked = offs_sb[:, (part * GATHER + lo) // 16 : (part * GATHER + hi) // 16]
-                nc.vector.tensor_copy(codes[:, lo:hi], x_codes[:].indirect(picked))
-                nc.vector.tensor_copy(scales[:, lo:hi], x_scales[:].indirect(picked))
+            picked = offs_sb[:, part * GATHER // 16 : (part + 1) * GATHER // 16]
+            nc.vector.tensor_copy(codes[:], x_codes[:].indirect(picked))
+            nc.vector.tensor_copy(scales[:], x_scales[:].indirect(picked))
             return codes, scales
 
-        slots = [gather(0, "slot_codes", "slot_scales", (0, C, 3 * C))]
+        slots = [gather(0, "slot_codes", "slot_scales")]
 
         def new_operand(name, columns):
             codes = ring.tile([P, columns], U32, name=f"{name}_codes", align_bytes=64)
@@ -199,7 +201,7 @@ def tile_moe_two_mlp_silu_kernel(tc, xT, w1, w2, gate, offs, dst, out):
 
         def first_layers(e, m_vector):
             stages = [interleave_w1(e, s, m_vector[s]) for s in range(HALVES)]
-            return [first_layer(e, stage, TWO if e + s >= EARLY else WHOLE) for s, stage in enumerate(stages)]
+            return [first_layer(e, stage, TWO if e >= EARLY else WHOLE) for stage in stages]
 
         for e in range(EARLY):
             accs = first_layers(e, (P, 2 * M_VECTOR - P) if e < 2 else (M_VECTOR, M_VECTOR))
@@ -209,7 +211,7 @@ def tile_moe_two_mlp_silu_kernel(tc, xT, w1, w2, gate, offs, dst, out):
                 interleave_w2(scopy, e, w2_stage, 0, HALVES)
                 h = silu(accs)
             else:
-                slots.append(gather(1, stage_tag(0, 0), "w1_raw0", (0, C, 3 * C)))
+                slots.append(gather(1, stage_tag(0, 0), "w1_raw0"))
                 h = silu(accs)
                 w2_stage = keep.tile([P, HALVES * 4 * N], BF16, name="w2_first", tag=stage_tag(0, 1), align_bytes=64)
                 interleave_w2(scopy, e, w2_stage, 0, HALVES)

from contextlib import ExitStack

import concourse.mybir as mybir
from concourse.masks import make_identity

K, T, E, C, H, N = 512, 768, 6, 128, 1024, 128
FLOPS = 2 * E * C * (K * H + H * N)
BYTES = 4 * (K * T + E * K * H + E * H * N + T + N * T) + 2 * 2 * 128 * (T // 16)

F32 = mybir.dt.float32
BF16 = mybir.dt.bfloat16
U32 = mybir.dt.uint32
U16 = mybir.dt.uint16
U8 = mybir.dt.uint8
FP8X4 = mybir.dt.float8_e4m3fn_x4
SILU = mybir.ActivationFunctionType.Silu
MULT = mybir.AluOpType.mult

P = 128
LAST = E - 1
EARLY = E - 2
HALF = 512
HALVES = H // HALF
GATHER = T // 2
GATES = T // P
M_VECTOR = 80
WHOLE, TWO, THREE = (0, HALF), (0, HALF // 2, HALF), (0, HALF // 2, 3 * HALF // 4, HALF)
M_VECTOR_LAST = 52


def tile_moe_two_mlp_silu_kernel(tc, xT, w1, w2, gate, offs, dst, out):
    nc = tc.nc
    with ExitStack() as ctx:
        lists = ctx.enter_context(tc.tile_pool(name="lists", bufs=1))
        keep = ctx.enter_context(tc.tile_pool(name="keep", bufs=1))
        ring = ctx.enter_context(tc.tile_pool(name="ring", bufs=3))
        psum_h = ctx.enter_context(tc.psum_pool(name="psum_h", bufs=4))
        psum_y = ctx.enter_context(tc.psum_pool(name="psum_y", bufs=2))
        psum_g = ctx.enter_context(tc.psum_pool(name="psum_g", bufs=2))

        offs_sb = lists.tile([P, T // 16], U16, name="offs_sb")
        dst_sb = lists.tile([P, T // 16], U16, name="dst_sb")

        x_raw = keep.tile([P, 4, T], F32, name="x_raw")
        w1_raw = [keep.tile([P, 4, H], F32, name=f"w1_raw{e}", align_bytes=64) for e in range(E)]
        w2_raw = [keep.tile([P, HALVES, 4, N], F32, name=f"w2_raw{e}", align_bytes=64) for e in range(E)]
        x_stage = keep.tile([P, 4 * T], BF16, name="x_stage", align_bytes=64)
        gate_row = keep.tile([P, GATES], F32, name="gate_row")
        gate_sb = keep.tile([P, T], F32, name="gate_sb")

        def load_w2(e):
            rows = w2[e].rearrange("(s p j) n -> p s j n", s=HALVES, j=4)
            if e == 0:
                nc.sync.dma_start(w2_raw[e][:], rows)
            else:
                for s in range(HALVES):
                    nc.sync.dma_start(w2_raw[e][:, s], rows[:, s])

        nc.scalar.dma_start(gate_row[:], gate[0:1, :].rearrange("o (p m) -> (o p) m", m=GATES))
        nc.sync.dma_start(x_raw[:], xT.rearrange("(p j) t -> p j t", j=4))
        nc.sync.dma_start(offs_sb[:], offs)
        for e in range(E):
            run, rows = w1_raw[e][:].rearrange("p j c -> p (j c)"), w1[e].rearrange("(p j) c -> p (j c)", j=4)
            cuts = (0, 4 * H - HALF, 4 * H) if e == LAST else (0, 4 * H)
            for lo, hi in zip(cuts, cuts[1:]):
                nc.sync.dma_start(run[:, lo:hi], rows[:, lo:hi])
            if e == 0:
                nc.sync.dma_start(dst_sb[:], dst)
            if e < EARLY:
                load_w2(e)
        for e in range(EARLY, E):
            load_w2(e)

        x_codes = keep.tile([P, T], U32, name="x_codes", align_bytes=64)
        x_scales = keep.tile([P, T], U8, name="x_scales", align_bytes=64)
        out_sb = keep.tile([P, T], F32, name="out_sb")
        ident = keep.tile([P, P], F32, name="ident")
        nc.gpsimd.memset(x_scales[:], 0)
        make_identity(nc, ident[:])

        def vcopy(to, source):
            nc.vector.tensor_copy(to, source)

        def scopy(to, source):
            nc.scalar.copy(to, source)

        def quantize(operand, stage, lo, hi):
            codes, scales = operand
            nc.vector.quantize_mx(
                out=codes[:, lo:hi].bitcast(FP8X4), scales=scales[:, lo:hi], in_=stage[:, 4 * lo : 4 * hi]
            )

        def matmul(acc, stationary, moving, start, stop):
            (w_codes, w_scales, w_lo), (a_codes, a_scales, a_lo) = stationary, moving
            nc.tensor.matmul_mx(
                out=acc,
                lhsT=w_codes[:, w_lo : w_lo + P].bitcast(FP8X4),
                lhsT_scale=w_scales[:, w_lo : w_lo + P],
                rhs=a_codes[:, a_lo : a_lo + C].bitcast(FP8X4),
                rhs_scale=a_scales[:, a_lo : a_lo + C],
                start=start,
                stop=stop,
            )

        for lo in range(0, GATES, 3):
            spread = psum_g.tile([P, 3, P], F32, name="spread")
            for m in range(3):
                nc.tensor.transpose(spread[:, m, :], gate_row[:, lo + m : lo + m + 1].to_broadcast([P, P]), ident[:])
            scopy(
                gate_sb[:].rearrange("p (n m) -> p n m", m=GATES)[:, :, lo : lo + 3],
                spread[:].rearrange("p m n -> p n m"),
            )

        vcopy(
            x_stage[:].rearrange("p (c i j) -> p c j i", i=2, j=4),
            x_raw[:].rearrange("p j (c i) -> p c j i", i=2),
        )
        for lo in range(0, T, T // 2):
            quantize((x_codes, x_scales), x_stage, lo, lo + T // 2)

        def gather(part, codes_tag, scales_tag):
            codes = keep.tile([P, GATHER], U32, name="slot_codes", tag=codes_tag, align_bytes=64)
            scales = keep.tile([P, GATHER], U8, name="slot_scales", tag=scales_tag, align_bytes=64)
            picked = offs_sb[:, part * GATHER // 16 : (part + 1) * GATHER // 16]
            nc.vector.tensor_copy(codes[:], x_codes[:].indirect(picked))
            nc.vector.tensor_copy(scales[:], x_scales[:].indirect(picked))
            return codes, scales

        slots = [gather(0, "slot_codes", "slot_scales")]

        def new_operand(name, columns):
            codes = ring.tile([P, columns], U32, name=f"{name}_codes", align_bytes=64)
            scales = ring.tile([P, columns], U8, name=f"{name}_scales", align_bytes=64)
            return codes, scales

        def stage_tag(e, s):
            return f"w1_stage{e}_{s}"

        def interleave_w1(e, s, m_vector):
            stage = keep.tile([P, 4 * HALF], BF16, name="w1_stage", tag=stage_tag(e, s), align_bytes=64)
            to = stage[:].rearrange("p (u v m j) -> p u m j v", u=2, v=2, j=4)
            source = w1_raw[e][:, :, s * HALF : (s + 1) * HALF].rearrange("p j (m u v) -> p u m j v", u=2, v=2)
            if m_vector < P:
                vcopy(to[:, :, :m_vector], source[:, :, :m_vector])
                scopy(to[:, :, m_vector:], source[:, :, m_vector:])
            elif e == LAST:
                for u in range(2):
                    vcopy(to[:, u], source[:, u])
            else:
                vcopy(to, source)
            return stage

        def first_layer(e, stage, cuts):
            w1_q = new_operand("w1", HALF)
            for lo, hi in zip(cuts, cuts[1:]):
                quantize(w1_q, stage, lo, hi)
            acc = psum_h.tile([P, 4, C], F32, name="acc_h")
            for t in range(4):
                matmul(acc[:, t, :], (*w1_q, P * t), (*slots[C * e // GATHER], C * e % GATHER), True, True)
            return acc

        def silu(accs):
            h = ring.tile([P, HALVES * 4 * C], BF16, name="h_stage", align_bytes=64)
            for s, acc in enumerate(accs):
                to = h[:, 4 * C * s : 4 * C * (s + 1)].rearrange("p (n t) -> p n t", t=4)
                nc.scalar.activation(to, acc[:].rearrange("p t n -> p n t"), SILU)
            return h

        def new_w2_stage():
            stage = ring.tile([P, HALVES * 4 * N], BF16, name="w2_stage", align_bytes=64)
            return stage

        def interleave_w2(copy, e, stage, first, stop):
            to = stage[:].rearrange("p (s c i j) -> p s c j i", s=HALVES, i=2, j=4)
            source = w2_raw[e][:].rearrange("p s j (c i) -> p s c j i", i=2)
            copy(to[:, first:stop], source[:, first:stop])

        def second_layer(w2_q, h_passes):
            acc = psum_y.tile([P, C], F32, name="acc_y")
            for s in range(HALVES):
                matmul(acc[:], (*w2_q, N * s), h_passes[s], s == 0, s == HALVES - 1)
            return acc

        def times_gate(e, acc, spent):
            y = spent[:, 2, HALF : HALF + C]
            nc.vector.tensor_tensor(y, acc[:], gate_sb[:, e * C : (e + 1) * C], MULT)
            return y

        def scatter(e, y):
            places = dst_sb[:, e * C // 16 : (e + 1) * C // 16]
            nc.vector.tensor_copy(out_sb[:].indirect(places), y)

        def empty(acc):
            y = ring.tile([P, C], F32, name="y")
            scopy(y[:], acc[:])
            return y[:]

        def scatter_times_gate(e, y):
            places = dst_sb[:, e * C // 16 : (e + 1) * C // 16]
            nc.vector.tensor_tensor(out_sb[:].indirect(places), y, gate_sb[:, e * C : (e + 1) * C], MULT)

        def first_layers(e, m_vector):
            stages = [interleave_w1(e, s, m_vector[s]) for s in range(HALVES)]
            return [first_layer(e, stage, TWO if e >= EARLY else WHOLE) for stage in stages]

        for e in range(EARLY):
            accs = first_layers(e, (P, 2 * M_VECTOR - P) if e < 2 else (M_VECTOR, M_VECTOR))
            if e > 0:
                scatter(e - 1, times_gate(e - 1, acc_y, w1_raw[e]))
                w2_stage = new_w2_stage()
                interleave_w2(scopy, e, w2_stage, 0, HALVES)
                h = silu(accs)
            else:
                slots.append(gather(1, stage_tag(0, 0), "w1_raw0"))
                h = silu(accs)
                w2_stage = keep.tile([P, HALVES * 4 * N], BF16, name="w2_first", tag=stage_tag(0, 1), align_bytes=64)
                interleave_w2(scopy, e, w2_stage, 0, HALVES)
            w2_q, h_q = new_operand("w2", HALVES * N), new_operand("h", HALVES * C)
            quantize(w2_q, w2_stage, 0, HALVES * N)
            quantize(h_q, h, 0, HALVES * C)
            acc_y = second_layer(w2_q, [(*h_q, C * s) for s in range(HALVES)])

        accs = first_layers(EARLY, (M_VECTOR, M_VECTOR))
        y = w1_raw[EARLY][:, 3, H - C :]
        scopy(y, acc_y[:])
        scatter_times_gate(EARLY - 1, y)
        h_before = silu(accs)
        stages = [interleave_w1(LAST, 0, P), interleave_w1(LAST, 1, M_VECTOR_LAST)]
        accs = [first_layer(LAST, stages[0], TWO), first_layer(LAST, stages[1], THREE)]
        late_codes = keep.tile([P, HALVES * C], U32, name="late_codes", tag=stage_tag(LAST, 1), align_bytes=64)
        late_scales = keep.tile([P, HALVES * C], U8, name="late_scales", align_bytes=64)
        h_before_q = (late_codes, late_scales)

        w2_before, w2_before_q = new_w2_stage(), new_operand("w2", HALVES * N)
        w2_last = new_w2_stage()
        for s in range(HALVES):
            interleave_w2(scopy, EARLY, w2_before, s, s + 1)
        quantize(w2_before_q, w2_before, 0, N)
        quantize(h_before_q, h_before, 0, HALVES * C)
        quantize(w2_before_q, w2_before, N, 2 * N)
        for s in range(HALVES):
            interleave_w2(vcopy, LAST, w2_last, s, s + 1)
        acc_before = second_layer(w2_before_q, [(*h_before_q, C * s) for s in range(HALVES)])

        h, h_q, w2_q = silu(accs), new_operand("h", HALVES * C), new_operand("w2", HALVES * N)
        quantize(w2_q, w2_last, 0, N)
        quantize(h_q, h, 0, C)
        quantize(w2_q, w2_last, N, 2 * N)
        quantize(h_q, h, C, 2 * C)
        scatter_times_gate(EARLY, empty(acc_before))
        scatter_times_gate(LAST, empty(second_layer(w2_q, [(*h_q, C * s) for s in range(HALVES)])))
        nc.sync.dma_start(out, out_sb[:])
